import numpy as np
import ml_dtypes


def mxq(x, axis, fmt="e4m3"):
    dtype, down = {"e4m3": (ml_dtypes.float8_e4m3fn, 7), "e5m2": (ml_dtypes.float8_e5m2, 14)}[fmt]
    v = np.moveaxis(np.asarray(x, np.float32).astype(ml_dtypes.bfloat16).astype(np.float64), axis, -1)
    blocks = v.reshape(v.shape[:-1] + (-1, 32))
    amax = np.abs(blocks).max(-1, keepdims=True)
    byte = np.maximum(np.where(amax > 0, np.frexp(amax)[1] - 1 + 127, 0) - down, 1)
    scale = np.exp2(byte - 127.0)
    codes = (blocks / scale).astype(np.float32).astype(dtype).astype(np.float64)
    return np.moveaxis((codes * scale).reshape(v.shape), -1, axis)


WIDE = False


def mx_kscale(k):
    if not WIDE:
        return np.ones(k)
    levels = np.array([10, -10, 5, -5, 0])
    if k % 512:
        return np.exp2(np.random.permutation(np.resize(levels, k // 32))).repeat(32)
    a = np.empty((k // 512, 16))
    for p in range(k // 512):
        a[p, :8] = np.random.permutation(np.resize(levels, 8))
        for g in range(8):
            far = levels[np.abs(levels - a[p, g]) >= 10]
            a[p, g + 8] = far[np.random.randint(len(far))]
    return np.exp2(a.ravel()).repeat(32)


def f64(x):
    return np.asarray(x).astype(np.float64)


def striped(idx):
    return np.tile(idx.reshape(-1, 16).T, (8, 1)).astype(np.uint16)


def unstriped(offs):
    return offs[:16].T.reshape(-1).astype(np.int64)


K, T, D, S, V, N = 1024, 2048, 2, 768, 384, 256


def setup_inputs():
    n = np.random.standard_normal
    s = mx_kscale(K)[:, None]
    return {
        "xT": (n((K, T)) * s).astype(np.float32),
        "w": (n((K, N)) / np.sqrt(K) / s).astype(np.float32),
        "b": (0.3 * n((N, 1))).astype(np.float32),
        "gate": np.tile(np.random.uniform(0.2, 1.0, (D, 1, V)) / np.sqrt(D), (1, N, 1)).astype(np.float32),
        "offs": striped(np.random.permutation(T)[:S]),
        "pos1": striped(np.random.permutation(S)[:V]),
        "pos2": striped(np.random.permutation(S)[:V]),
    }


def reference(xT, w, b, gate, offs, pos1, pos2):
    idx = unstriped(offs)
    xq = mxq(f64(xT)[:, idx], 0, "e4m3")
    y = mxq(f64(w), 0, "e4m3").T @ xq
    y = y + f64(b)
    return sum(f64(gate[d]) * y[:, unstriped(p)] for d, p in enumerate((pos1, pos2)))

@@ -1,0 +1,165 @@
+from contextlib import ExitStack
+
+import concourse.mybir as mybir
+
+K, T, D, S, V, N = 1024, 2048, 2, 768, 384, 256
+FLOPS = 2 * K * N * S
+
+F32 = mybir.dt.float32
+BF16 = mybir.dt.bfloat16
+U32 = mybir.dt.uint32
+U16 = mybir.dt.uint16
+U8 = mybir.dt.uint8
+FP8X4 = mybir.dt.float8_e4m3fn_x4
+IDENTITY = mybir.ActivationFunctionType.Identity
+ADD = mybir.AluOpType.add
+MULT = mybir.AluOpType.mult
+
+P = 128
+PACK = 4
+K_PASS = P * PACK
+PASSES = K // K_PASS
+SLICE = 256
+SLICES = S // SLICE
+BLOCKS = N // P
+STRIPE = 16
+
+
+def tile_picked_sub_lin_bias_sub_e_kernel(tc, xT, w, b, gate, offs, pos1, pos2, out):
+    nc = tc.nc
+    with ExitStack() as ctx:
+        keep = ctx.enter_context(tc.tile_pool(name="keep", bufs=1))
+        psum = ctx.enter_context(tc.psum_pool(name="psum", bufs=1))
+
+        offs_sb = keep.tile([P, S // STRIPE], U16, name="offs_sb")
+        pos_sb = [keep.tile([P, V // STRIPE], U16, name=f"pos_sb{d}") for d in range(D)]
+
+        warm = keep.tile([P, 8], F32, name="warm")
+        warm_out = keep.tile([P, 8], F32, name="warm_out")
+        nc.gpsimd.memset(warm[:], 0.0)
+        nc.scalar.activation(warm_out[:], warm[:], IDENTITY)
+
+        x_rows = xT.rearrange("(a p j) t -> a j p t", p=P, j=PACK)
+        order = [(1, 2), (0, 0), (0, 1), (0, 2), (0, 3), (1, 0), (1, 1), (1, 3)]
+        plane = {}
+        for n, (a, j) in enumerate(order):
+            plane[a, j] = keep.tile([P, T], F32, name=f"plane{a}{j}")
+            nc.sync.dma_start(plane[a, j][:], x_rows[a, j])
+            if n == 0:
+                nc.sync.dma_start(offs_sb[:], offs)
+        w_raw = []
+        for a in range(PASSES):
+            w_raw.append(keep.tile([P, PACK, N], F32, name=f"w_raw{a}"))
+            nc.sync.dma_start(w_raw[a][:], w[a * K_PASS : (a + 1) * K_PASS, :].rearrange("(p j) n -> p j n", j=PACK))
+        bias = keep.tile([P, BLOCKS], F32, name="bias")
+        with nc.allow_non_contiguous_dma(reason="one bias value a partition and block"):
+            nc.sync.dma_start(bias[:], b.rearrange("(h p) o -> p (h o)", p=P))
+        nc.sync.dma_start(pos_sb[0][:], pos1)
+        nc.sync.dma_start(pos_sb[1][:], pos2)
+        gate_sb = []
+        for h in range(BLOCKS):
+            gate_sb.append(keep.tile([P, D, V], F32, name=f"gate_sb{h}"))
+            nc.sync.dma_start(gate_sb[h][:], gate[:, h * P : (h + 1) * P, :].rearrange("d p v -> p d v"))
+
+        def offsets(s):
+            return offs_sb[:, s * SLICE // STRIPE : (s + 1) * SLICE // STRIPE]
+
+        def cols(s):
+            return slice(s * SLICE, (s + 1) * SLICE)
+
+        x_bf = {(a, s): keep.tile([P, SLICE, PACK], BF16, name=f"x_bf{a}{s}", align_bytes=64) for a in range(PASSES) for s in range(SLICES)}
+        x_codes = {(a, s): keep.tile([P, SLICE], U32, name=f"x_codes{a}{s}", align_bytes=64) for a in range(PASSES) for s in range(SLICES)}
+        x_scales = {(a, s): keep.tile([P, SLICE], U8, name=f"x_scales{a}{s}", align_bytes=64) for a in range(PASSES) for s in range(SLICES)}
+        w_bf = {(a, h): keep.tile([P, P, PACK], BF16, name=f"w_bf{a}{h}", align_bytes=64) for a in range(PASSES) for h in range(BLOCKS)}
+        w_codes = {(a, h): keep.tile([P, P], U32, name=f"w_codes{a}{h}", align_bytes=64) for a in range(PASSES) for h in range(BLOCKS)}
+        w_scales = {(a, h): keep.tile([P, P], U8, name=f"w_scales{a}{h}", align_bytes=64) for a in range(PASSES) for h in range(BLOCKS)}
+        picked0 = keep.tile([P, PACK, S], F32, name="picked0")
+        picked1 = keep.tile([P, 2, S], F32, name="picked1")
+        acc = {(h, s): psum.tile([P, SLICE], F32, name=f"acc{h}{s}") for h in range(BLOCKS) for s in range(SLICES)}
+        y = [keep.tile([P, S], F32, name=f"y{h}") for h in range(BLOCKS)]
+        term = {(h, d): keep.tile([P, V], F32, name=f"term{h}{d}") for h in range(BLOCKS) for d in range(D)}
+        result = [keep.tile([P, V], F32, name=f"result{h}") for h in range(BLOCKS)]
+
+        def interleave(dst, src):
+            nc.scalar.copy(dst.rearrange("p (c i) t -> p c t i", i=4), src.rearrange("p t (c i) -> p c t i", i=4))
+
+        def quantize(codes, scales, grouped):
+            nc.vector.quantize_mx(out=codes[:].bitcast(FP8X4), scales=scales[:], in_=grouped[:].rearrange("p c t -> p (c t)"))
+
+        def gather_stepped(a, j, s):
+            nc.vector.tensor_copy(x_bf[a, s][:, :, j], plane[a, j][:].indirect(offsets(s)))
+
+        def quantize_x(a, s):
+            quantize(x_codes[a, s], x_scales[a, s], x_bf[a, s])
+
+        def round_w(a, h):
+            interleave(w_bf[a, h][:], w_raw[a][:, :, h * P : (h + 1) * P])
+
+        def quantize_w(a, h):
+            quantize(w_codes[a, h], w_scales[a, h], w_bf[a, h])
+
+        def multiply(a, h, s):
+            nc.tensor.matmul_mx(
+                out=acc[h, s][:],
+                lhsT=w_codes[a, h][:].bitcast(FP8X4),
+                lhsT_scale=w_scales[a, h][:],
+                rhs=x_codes[a, s][:].bitcast(FP8X4),
+                rhs_scale=x_scales[a, s][:],
+                start=(a == 0),
+                stop=(a == PASSES - 1),
+            )
+
+        def weighted(h, d):
+            nc.vector.tensor_tensor(term[h, d][:], y[h][:].indirect(pos_sb[d][:]), gate_sb[h][:, d, :], MULT)
+
+        def finish(h):
+            nc.vector.tensor_tensor(result[h][:], term[h, 0][:], term[h, 1][:], ADD)
+            nc.sync.dma_start(out[h * P : (h + 1) * P, :], result[h][:])
+
+        for s in range(SLICES):
+            gather_stepped(1, 2, s)
+        for j in range(PACK - 1):
+            nc.vector.tensor_copy(picked0[:, j, :], plane[0, j][:].indirect(offs_sb[:]))
+        for s in range(SLICES):
+            nc.vector.tensor_copy(picked0[:, PACK - 1, cols(s)], plane[0, PACK - 1][:].indirect(offsets(s)))
+            interleave(x_bf[0, s][:], picked0[:, :, cols(s)])
+        nc.vector.tensor_copy(picked1[:, 0, :], plane[1, 0][:].indirect(offs_sb[:]))
+        quantize_x(0, 0)
+        for s in range(SLICES):
+            nc.vector.tensor_copy(picked1[:, 1, cols(s)], plane[1, 1][:].indirect(offsets(s)))
+            interleave(x_bf[1, s][:, :, 0:2], picked1[:, :, cols(s)])
+        quantize_x(0, 1)
+        quantize_x(0, 2)
+
+        gather_stepped(1, 3, 0)
+        gather_stepped(1, 3, 1)
+        quantize_x(1, 0)
+        round_w(0, 0)
+        gather_stepped(1, 3, 2)
+        quantize_x(1, 1)
+        quantize_w(0, 0)
+        round_w(0, 1)
+        round_w(1, 0)
+        for s in range(SLICES):
+            multiply(0, 0, s)
+        quantize_x(1, 2)
+        quantize_w(1, 0)
+        round_w(1, 1)
+        for s in range(SLICES):
+            multiply(1, 0, s)
+        quantize_w(0, 1)
+        quantize_w(1, 1)
+        for s in range(SLICES - 1):
+            nc.scalar.activation(y[0][:, cols(s)], acc[0, s][:], IDENTITY, bias=bias[:, 0:1])
+        nc.vector.tensor_scalar(y[0][:, cols(SLICES - 1)], acc[0, SLICES - 1][:], bias[:, 0:1], None, ADD)
+        for a in range(PASSES):
+            for s in range(SLICES):
+                multiply(a, 1, s)
+        for s in range(SLICES):
+            nc.scalar.activation(y[1][:, cols(s)], acc[1, s][:], IDENTITY, bias=bias[:, 1:2])
+        weighted(0, 0)
+        weighted(0, 1)
+        weighted(1, 0)
+        finish(0)
+        weighted(1, 1)
+        finish(1)

@@ -1,6 +1,7 @@
 from contextlib import ExitStack
 
 import concourse.mybir as mybir
+from concourse.masks import make_identity
 
 K, T, D, S, V, N = 1024, 2048, 2, 768, 384, 256
 FLOPS = 2 * K * N * S
@@ -43,7 +44,7 @@ def tile_picked_sub_lin_bias_sub_e_kernel(tc, xT, w, b, gate, offs, pos1, pos2, 
         order = [(1, 2), (0, 0), (0, 1), (0, 2), (0, 3), (1, 0), (1, 1), (1, 3)]
         plane = {}
         for n, (a, j) in enumerate(order):
-            plane[a, j] = keep.tile([P, T], F32, name=f"plane{a}{j}")
+            plane[a, j] = keep.tile([P, T], F32, name=f"plane{a}{j}", align_bytes=64)
             nc.sync.dma_start(plane[a, j][:], x_rows[a, j])
             if n == 0:
                 nc.sync.dma_start(offs_sb[:], offs)
@@ -55,11 +56,12 @@ def tile_picked_sub_lin_bias_sub_e_kernel(tc, xT, w, b, gate, offs, pos1, pos2, 
         with nc.allow_non_contiguous_dma(reason="one bias value a partition and block"):
             nc.sync.dma_start(bias[:], b.rearrange("(h p) o -> p (h o)", p=P))
         nc.sync.dma_start(pos_sb[0][:], pos1)
-        nc.sync.dma_start(pos_sb[1][:], pos2)
         gate_sb = []
         for h in range(BLOCKS):
             gate_sb.append(keep.tile([P, D, V], F32, name=f"gate_sb{h}"))
             nc.sync.dma_start(gate_sb[h][:], gate[:, h * P : (h + 1) * P, :].rearrange("d p v -> p d v"))
+            if h == 0:
+                nc.sync.dma_start(pos_sb[1][:], pos2)
 
         def offsets(s):
             return offs_sb[:, s * SLICE // STRIPE : (s + 1) * SLICE // STRIPE]
@@ -67,14 +69,16 @@ def tile_picked_sub_lin_bias_sub_e_kernel(tc, xT, w, b, gate, offs, pos1, pos2, 
         def cols(s):
             return slice(s * SLICE, (s + 1) * SLICE)
 
-        x_bf = {(a, s): keep.tile([P, SLICE, PACK], BF16, name=f"x_bf{a}{s}", align_bytes=64) for a in range(PASSES) for s in range(SLICES)}
-        x_codes = {(a, s): keep.tile([P, SLICE], U32, name=f"x_codes{a}{s}", align_bytes=64) for a in range(PASSES) for s in range(SLICES)}
-        x_scales = {(a, s): keep.tile([P, SLICE], U8, name=f"x_scales{a}{s}", align_bytes=64) for a in range(PASSES) for s in range(SLICES)}
-        w_bf = {(a, h): keep.tile([P, P, PACK], BF16, name=f"w_bf{a}{h}", align_bytes=64) for a in range(PASSES) for h in range(BLOCKS)}
-        w_codes = {(a, h): keep.tile([P, P], U32, name=f"w_codes{a}{h}", align_bytes=64) for a in range(PASSES) for h in range(BLOCKS)}
-        w_scales = {(a, h): keep.tile([P, P], U8, name=f"w_scales{a}{h}", align_bytes=64) for a in range(PASSES) for h in range(BLOCKS)}
-        picked0 = keep.tile([P, PACK, S], F32, name="picked0")
-        picked1 = keep.tile([P, 2, S], F32, name="picked1")
+        x_bf_rest = keep.tile([P, S - SLICE, PACK], BF16, name="x_bf_rest", align_bytes=64)
+        x_bf = {(a, s): keep.tile([P, SLICE, PACK], BF16, name=f"x_bf{a}{s}", align_bytes=64)[:] for a, s in ((0, 0), (1, 0), (1, 1), (1, 2))}
+        x_bf[0, 1], x_bf[0, 2] = x_bf_rest[:, :SLICE], x_bf_rest[:, SLICE:]
+        x_codes = {}
+        x_scales = {}
+        w_bf_first = [keep.tile([P, P, PACK], BF16, name=f"w_bf_first{a}", align_bytes=64) for a in range(PASSES)]
+        w_bf_second = keep.tile([P, PASSES, P, PACK], BF16, name="w_bf_second", align_bytes=64)
+        w_codes = [keep.tile([P, PASSES, P], U32, name=f"w_codes{h}", align_bytes=64) for h in range(BLOCKS)]
+        w_scales = [keep.tile([P, PASSES, P], U8, name=f"w_scales{h}", align_bytes=64) for h in range(BLOCKS)]
+        picked = {(a, u): keep.tile([P, 2, S], F32, name=f"picked{a}{u}") for a, u in ((0, 0), (0, 1), (1, 0))}
         acc = {(h, s): psum.tile([P, SLICE], F32, name=f"acc{h}{s}") for h in range(BLOCKS) for s in range(SLICES)}
         y = [keep.tile([P, S], F32, name=f"y{h}") for h in range(BLOCKS)]
         term = {(h, d): keep.tile([P, V], F32, name=f"term{h}{d}") for h in range(BLOCKS) for d in range(D)}
@@ -84,82 +88,99 @@ def tile_picked_sub_lin_bias_sub_e_kernel(tc, xT, w, b, gate, offs, pos1, pos2, 
             nc.scalar.copy(dst.rearrange("p (c i) t -> p c t i", i=4), src.rearrange("p t (c i) -> p c t i", i=4))
 
         def quantize(codes, scales, grouped):
-            nc.vector.quantize_mx(out=codes[:].bitcast(FP8X4), scales=scales[:], in_=grouped[:].rearrange("p c t -> p (c t)"))
+            nc.vector.quantize_mx(out=codes.bitcast(FP8X4), scales=scales, in_=grouped.rearrange("p c t -> p (c t)"))
 
         def gather_stepped(a, j, s):
             nc.vector.tensor_copy(x_bf[a, s][:, :, j], plane[a, j][:].indirect(offsets(s)))
 
-        def quantize_x(a, s):
-            quantize(x_codes[a, s], x_scales[a, s], x_bf[a, s])
+        def quantize_x(a, slices, grouped, tag):
+            width = SLICE * len(slices)
+            codes = keep.tile([P, width], U32, name=f"x_codes{a}{slices[0]}", tag=tag, align_bytes=64)
+            scales = keep.tile([P, width], U8, name=f"x_scales{a}{slices[0]}", align_bytes=64)
+            quantize(codes[:], scales[:], grouped)
+            for n, s in enumerate(slices):
+                x_codes[a, s], x_scales[a, s] = codes[:, cols(n)], scales[:, cols(n)]
 
         def round_w(a, h):
-            interleave(w_bf[a, h][:], w_raw[a][:, :, h * P : (h + 1) * P])
+            interleave(w_bf_first[a][:] if h == 0 else w_bf_second[:, a], w_raw[a][:, :, h * P : (h + 1) * P])
 
         def quantize_w(a, h):
-            quantize(w_codes[a, h], w_scales[a, h], w_bf[a, h])
+            quantize(w_codes[h][:, a], w_scales[h][:, a], w_bf_first[a][:])
+
+        def quantize_w_passes(h):
+            quantize(
+                w_codes[h][:].rearrange("p a m -> p (a m)"),
+                w_scales[h][:].rearrange("p a m -> p (a m)"),
+                w_bf_second[:].rearrange("p a m t -> p (a m) t"),
+            )
 
         def multiply(a, h, s):
             nc.tensor.matmul_mx(
                 out=acc[h, s][:],
-                lhsT=w_codes[a, h][:].bitcast(FP8X4),
-                lhsT_scale=w_scales[a, h][:],
-                rhs=x_codes[a, s][:].bitcast(FP8X4),
-                rhs_scale=x_scales[a, s][:],
+                lhsT=w_codes[h][:, a].bitcast(FP8X4),
+                lhsT_scale=w_scales[h][:, a],
+                rhs=x_codes[a, s].bitcast(FP8X4),
+                rhs_scale=x_scales[a, s],
                 start=(a == 0),
                 stop=(a == PASSES - 1),
             )
 
-        def weighted(h, d):
-            nc.vector.tensor_tensor(term[h, d][:], y[h][:].indirect(pos_sb[d][:]), gate_sb[h][:, d, :], MULT)
+        def weighted(h, d, v0, v1):
+            where = pos_sb[d][:, v0 // STRIPE : v1 // STRIPE]
+            nc.vector.tensor_tensor(term[h, d][:, v0:v1], y[h][:].indirect(where), gate_sb[h][:, d, v0:v1], MULT)
 
-        def finish(h):
-            nc.vector.tensor_tensor(result[h][:], term[h, 0][:], term[h, 1][:], ADD)
-            nc.sync.dma_start(out[h * P : (h + 1) * P, :], result[h][:])
+        def finish(h, v0, v1):
+            nc.vector.tensor_tensor(result[h][:, v0:v1], term[h, 0][:, v0:v1], term[h, 1][:, v0:v1], ADD)
+            nc.sync.dma_start(out[h * P : (h + 1) * P, v0:v1], result[h][:, v0:v1])
+
+        def gather_pair(a, u):
+            nc.vector.tensor_copy(picked[a, u][:, 0, :], plane[a, 2 * u][:].indirect(offs_sb[:]))
+            for s in range(SLICES):
+                nc.vector.tensor_copy(picked[a, u][:, 1, cols(s)], plane[a, 2 * u + 1][:].indirect(offsets(s)))
+                nc.scalar.copy(x_bf[a, s][:, :, 2 * u : 2 * u + 2], picked[a, u][:, :, cols(s)].rearrange("p t c -> p c t"))
 
         for s in range(SLICES):
             gather_stepped(1, 2, s)
-        for j in range(PACK - 1):
-            nc.vector.tensor_copy(picked0[:, j, :], plane[0, j][:].indirect(offs_sb[:]))
-        for s in range(SLICES):
-            nc.vector.tensor_copy(picked0[:, PACK - 1, cols(s)], plane[0, PACK - 1][:].indirect(offsets(s)))
-            interleave(x_bf[0, s][:], picked0[:, :, cols(s)])
-        nc.vector.tensor_copy(picked1[:, 0, :], plane[1, 0][:].indirect(offs_sb[:]))
-        quantize_x(0, 0)
-        for s in range(SLICES):
-            nc.vector.tensor_copy(picked1[:, 1, cols(s)], plane[1, 1][:].indirect(offsets(s)))
-            interleave(x_bf[1, s][:, :, 0:2], picked1[:, :, cols(s)])
-        quantize_x(0, 1)
-        quantize_x(0, 2)
+        gather_pair(0, 0)
+        gather_pair(0, 1)
+        gather_pair(1, 0)
+        quantize_x(0, [0], x_bf[0, 0], "x_codes00")
+        quantize_x(0, [1, 2], x_bf_rest[:], "plane10")
 
-        gather_stepped(1, 3, 0)
-        gather_stepped(1, 3, 1)
-        quantize_x(1, 0)
+        identity = keep.tile([P, P], F32, name="identity")
+        make_identity(nc, identity[:])
+        spare = psum.tile([P, 4, P], F32, name="spare")
+        for n in range(26):
+            nc.tensor.transpose(spare[:, n % 4, :], picked[1, 0][:, 1, 0:P], identity[:])
+
+        for s in range(SLICES):
+            gather_stepped(1, 3, s)
         round_w(0, 0)
-        gather_stepped(1, 3, 2)
-        quantize_x(1, 1)
         quantize_w(0, 0)
         round_w(0, 1)
         round_w(1, 0)
-        for s in range(SLICES):
-            multiply(0, 0, s)
-        quantize_x(1, 2)
-        quantize_w(1, 0)
         round_w(1, 1)
         for s in range(SLICES):
+            multiply(0, 0, s)
+        quantize_x(1, [0], x_bf[1, 0], "w_bf_first0")
+        quantize_x(1, [1], x_bf[1, 1], "x_codes11")
+        quantize_w(1, 0)
+        quantize_x(1, [2], x_bf[1, 2], "w_bf_first1")
+        for s in range(SLICES):
             multiply(1, 0, s)
-        quantize_w(0, 1)
-        quantize_w(1, 1)
+        quantize_w_passes(1)
         for s in range(SLICES - 1):
             nc.scalar.activation(y[0][:, cols(s)], acc[0, s][:], IDENTITY, bias=bias[:, 0:1])
         nc.vector.tensor_scalar(y[0][:, cols(SLICES - 1)], acc[0, SLICES - 1][:], bias[:, 0:1], None, ADD)
-        for a in range(PASSES):
-            for s in range(SLICES):
-                multiply(a, 1, s)
         for s in range(SLICES):
+            for a in range(PASSES):
+                multiply(a, 1, s)
             nc.scalar.activation(y[1][:, cols(s)], acc[1, s][:], IDENTITY, bias=bias[:, 1:2])
-        weighted(0, 0)
-        weighted(0, 1)
-        weighted(1, 0)
-        finish(0)
-        weighted(1, 1)
-        finish(1)
+        weighted(0, 0, 0, V)
+        weighted(0, 1, 0, V)
+        weighted(1, 0, 0, V)
+        finish(0, 0, V)
+        weighted(1, 1, 0, 256)
+        weighted(1, 1, 256, V)
+        finish(1, 0, 256)
+        finish(1, 256, V)

@@ -1,7 +1,6 @@
 from contextlib import ExitStack
 
 import concourse.mybir as mybir
-from concourse.masks import make_identity
 
 K, T, D, S, V, N = 1024, 2048, 2, 768, 384, 256
 FLOPS = 2 * K * N * S
@@ -41,141 +40,135 @@ def tile_picked_sub_lin_bias_sub_e_kernel(tc, xT, w, b, gate, offs, pos1, pos2, 
         nc.scalar.activation(warm_out[:], warm[:], IDENTITY)
 
         x_rows = xT.rearrange("(a p j) t -> a j p t", p=P, j=PACK)
-        order = [(1, 2), (0, 0), (0, 1), (0, 2), (0, 3), (1, 0), (1, 1), (1, 3)]
+        order = [(a, j) for a in range(PASSES) for j in range(PACK)]
         plane = {}
         for n, (a, j) in enumerate(order):
             plane[a, j] = keep.tile([P, T], F32, name=f"plane{a}{j}", align_bytes=64)
             nc.sync.dma_start(plane[a, j][:], x_rows[a, j])
             if n == 0:
                 nc.sync.dma_start(offs_sb[:], offs)
-        w_raw = []
-        for a in range(PASSES):
-            w_raw.append(keep.tile([P, PACK, N], F32, name=f"w_raw{a}"))
-            nc.sync.dma_start(w_raw[a][:], w[a * K_PASS : (a + 1) * K_PASS, :].rearrange("(p j) n -> p j n", j=PACK))
+        w_rows = w.rearrange("(a p j) n -> a p j n", p=P, j=PACK)
+        w_raw = {}
+        for h in range(BLOCKS):
+            for a in range(PASSES):
+                w_raw[a, h] = keep.tile([P, PACK, P], F32, name=f"w_raw{a}{h}")
+                nc.sync.dma_start(w_raw[a, h][:], w_rows[a][:, :, h * P : (h + 1) * P])
         bias = keep.tile([P, BLOCKS], F32, name="bias")
         with nc.allow_non_contiguous_dma(reason="one bias value a partition and block"):
             nc.sync.dma_start(bias[:], b.rearrange("(h p) o -> p (h o)", p=P))
         nc.sync.dma_start(pos_sb[0][:], pos1)
-        gate_sb = []
-        for h in range(BLOCKS):
-            gate_sb.append(keep.tile([P, D, V], F32, name=f"gate_sb{h}"))
-            nc.sync.dma_start(gate_sb[h][:], gate[:, h * P : (h + 1) * P, :].rearrange("d p v -> p d v"))
-            if h == 0:
-                nc.sync.dma_start(pos_sb[1][:], pos2)
+        gate_sb = keep.tile([P, D, V], F32, name="gate_sb")
+        nc.sync.dma_start(gate_sb[:], gate[:, :P, :].rearrange("d p v -> p d v"))
+        nc.sync.dma_start(pos_sb[1][:], pos2)
 
-        def offsets(s):
-            return offs_sb[:, s * SLICE // STRIPE : (s + 1) * SLICE // STRIPE]
+        def offsets(c0, c1):
+            return offs_sb[:, c0 // STRIPE : c1 // STRIPE]
 
         def cols(s):
             return slice(s * SLICE, (s + 1) * SLICE)
 
-        x_bf_rest = keep.tile([P, S - SLICE, PACK], BF16, name="x_bf_rest", align_bytes=64)
-        x_bf = {(a, s): keep.tile([P, SLICE, PACK], BF16, name=f"x_bf{a}{s}", align_bytes=64)[:] for a, s in ((0, 0), (1, 0), (1, 1), (1, 2))}
-        x_bf[0, 1], x_bf[0, 2] = x_bf_rest[:, :SLICE], x_bf_rest[:, SLICE:]
-        x_codes = {}
-        x_scales = {}
+        x_bf_first = [keep.tile([P, SLICE, PACK], BF16, name=f"x_bf_first{a}", align_bytes=64) for a in range(PASSES)]
+        x_bf_rest = [keep.tile([P, S - SLICE, PACK], BF16, name=f"x_bf_rest{a}", align_bytes=64) for a in range(PASSES)]
+        x_bf = {}
+        for a in range(PASSES):
+            x_bf[a, 0], x_bf[a, 1], x_bf[a, 2] = x_bf_first[a][:], x_bf_rest[a][:, :SLICE], x_bf_rest[a][:, SLICE:]
         w_bf_first = [keep.tile([P, P, PACK], BF16, name=f"w_bf_first{a}", align_bytes=64) for a in range(PASSES)]
-        w_bf_second = keep.tile([P, PASSES, P, PACK], BF16, name="w_bf_second", align_bytes=64)
         w_codes = [keep.tile([P, PASSES, P], U32, name=f"w_codes{h}", align_bytes=64) for h in range(BLOCKS)]
         w_scales = [keep.tile([P, PASSES, P], U8, name=f"w_scales{h}", align_bytes=64) for h in range(BLOCKS)]
-        picked = {(a, u): keep.tile([P, 2, S], F32, name=f"picked{a}{u}") for a, u in ((0, 0), (0, 1), (1, 0))}
-        acc = {(h, s): psum.tile([P, SLICE], F32, name=f"acc{h}{s}") for h in range(BLOCKS) for s in range(SLICES)}
+        picked = {(0, u): keep.tile([P, 2, S], F32, name=f"picked0{u}") for u in range(2)}
+        picked[1, 0] = keep.tile([P, 3, S], F32, name="picked10")
         y = [keep.tile([P, S], F32, name=f"y{h}") for h in range(BLOCKS)]
         term = {(h, d): keep.tile([P, V], F32, name=f"term{h}{d}") for h in range(BLOCKS) for d in range(D)}
         result = [keep.tile([P, V], F32, name=f"result{h}") for h in range(BLOCKS)]
 
-        def interleave(dst, src):
-            nc.scalar.copy(dst.rearrange("p (c i) t -> p c t i", i=4), src.rearrange("p t (c i) -> p c t i", i=4))
+        def interleave(copy, dst, src):
+            copy(dst.rearrange("p (c i) t -> p c t i", i=4), src.rearrange("p t (c i) -> p c t i", i=4))
 
         def quantize(codes, scales, grouped):
             nc.vector.quantize_mx(out=codes.bitcast(FP8X4), scales=scales, in_=grouped.rearrange("p c t -> p (c t)"))
 
-        def gather_stepped(a, j, s):
-            nc.vector.tensor_copy(x_bf[a, s][:, :, j], plane[a, j][:].indirect(offsets(s)))
+        def packed(name, width, tag):
+            codes = keep.tile([P, width], U32, name=f"{name}_codes", tag=tag, align_bytes=64)
+            scales = keep.tile([P, width], U8, name=f"{name}_scales", align_bytes=64)
+            return codes, scales
 
-        def quantize_x(a, slices, grouped, tag):
-            width = SLICE * len(slices)
-            codes = keep.tile([P, width], U32, name=f"x_codes{a}{slices[0]}", tag=tag, align_bytes=64)
-            scales = keep.tile([P, width], U8, name=f"x_scales{a}{slices[0]}", align_bytes=64)
-            quantize(codes[:], scales[:], grouped)
-            for n, s in enumerate(slices):
-                x_codes[a, s], x_scales[a, s] = codes[:, cols(n)], scales[:, cols(n)]
-
-        def round_w(a, h):
-            interleave(w_bf_first[a][:] if h == 0 else w_bf_second[:, a], w_raw[a][:, :, h * P : (h + 1) * P])
-
-        def quantize_w(a, h):
-            quantize(w_codes[h][:, a], w_scales[h][:, a], w_bf_first[a][:])
-
-        def quantize_w_passes(h):
-            quantize(
-                w_codes[h][:].rearrange("p a m -> p (a m)"),
-                w_scales[h][:].rearrange("p a m -> p (a m)"),
-                w_bf_second[:].rearrange("p a m t -> p (a m) t"),
-            )
-
-        def multiply(a, h, s):
+        def multiply(acc, a, h, operand, c0, c1):
+            codes, scales = operand
             nc.tensor.matmul_mx(
-                out=acc[h, s][:],
+                out=acc,
                 lhsT=w_codes[h][:, a].bitcast(FP8X4),
                 lhsT_scale=w_scales[h][:, a],
-                rhs=x_codes[a, s].bitcast(FP8X4),
-                rhs_scale=x_scales[a, s],
+                rhs=codes[:, c0:c1].bitcast(FP8X4),
+                rhs_scale=scales[:, c0:c1],
                 start=(a == 0),
                 stop=(a == PASSES - 1),
             )
 
         def weighted(h, d, v0, v1):
             where = pos_sb[d][:, v0 // STRIPE : v1 // STRIPE]
-            nc.vector.tensor_tensor(term[h, d][:, v0:v1], y[h][:].indirect(where), gate_sb[h][:, d, v0:v1], MULT)
+            nc.vector.tensor_tensor(term[h, d][:, v0:v1], y[h][:].indirect(where), gate_sb[:, d, v0:v1], MULT)
 
         def finish(h, v0, v1):
             nc.vector.tensor_tensor(result[h][:, v0:v1], term[h, 0][:, v0:v1], term[h, 1][:, v0:v1], ADD)
             nc.sync.dma_start(out[h * P : (h + 1) * P, v0:v1], result[h][:, v0:v1])
 
+        def round_slots(dst, j0, src):
+            nc.scalar.copy(dst[:, :, j0 : j0 + src.shape[1]], src.rearrange("p t c -> p c t"))
+
         def gather_pair(a, u):
             nc.vector.tensor_copy(picked[a, u][:, 0, :], plane[a, 2 * u][:].indirect(offs_sb[:]))
             for s in range(SLICES):
-                nc.vector.tensor_copy(picked[a, u][:, 1, cols(s)], plane[a, 2 * u + 1][:].indirect(offsets(s)))
-                nc.scalar.copy(x_bf[a, s][:, :, 2 * u : 2 * u + 2], picked[a, u][:, :, cols(s)].rearrange("p t c -> p c t"))
+                nc.vector.tensor_copy(picked[a, u][:, 1, cols(s)], plane[a, 2 * u + 1][:].indirect(offsets(s * SLICE, (s + 1) * SLICE)))
+                if (a, s) != (1, 0):
+                    round_slots(x_bf[a, s], 2 * u, picked[a, u][:, :2, cols(s)])
 
-        for s in range(SLICES):
-            gather_stepped(1, 2, s)
+        def gather_rest(j):
+            nc.vector.tensor_copy(x_bf_rest[1][:, :, j], plane[1, j][:].indirect(offsets(SLICE, S)))
+
         gather_pair(0, 0)
         gather_pair(0, 1)
         gather_pair(1, 0)
-        quantize_x(0, [0], x_bf[0, 0], "x_codes00")
-        quantize_x(0, [1, 2], x_bf_rest[:], "plane10")
+        first = {0: packed("first0", SLICE, "first0_codes")}
+        rest = {0: packed("rest0", S - SLICE, "plane10")}
+        quantize(first[0][0][:], first[0][1][:], x_bf_first[0][:])
+        quantize(rest[0][0][:], rest[0][1][:], x_bf_rest[0][:])
 
-        identity = keep.tile([P, P], F32, name="identity")
-        make_identity(nc, identity[:])
-        spare = psum.tile([P, 4, P], F32, name="spare")
-        for n in range(26):
-            nc.tensor.transpose(spare[:, n % 4, :], picked[1, 0][:, 1, 0:P], identity[:])
+        nc.vector.tensor_copy(picked[1, 0][:, 2, cols(0)], plane[1, 2][:].indirect(offsets(0, SLICE)))
+        round_slots(x_bf[1, 0], 0, picked[1, 0][:, :, cols(0)])
+        gather_rest(2)
+        gather_rest(3)
+        for a in range(PASSES):
+            interleave(nc.scalar.copy, w_bf_first[a][:], w_raw[a, 0][:])
 
-        for s in range(SLICES):
-            gather_stepped(1, 3, s)
-        round_w(0, 0)
-        quantize_w(0, 0)
-        round_w(0, 1)
-        round_w(1, 0)
-        round_w(1, 1)
-        for s in range(SLICES):
-            multiply(0, 0, s)
-        quantize_x(1, [0], x_bf[1, 0], "w_bf_first0")
-        quantize_x(1, [1], x_bf[1, 1], "x_codes11")
-        quantize_w(1, 0)
-        quantize_x(1, [2], x_bf[1, 2], "w_bf_first1")
-        for s in range(SLICES):
-            multiply(1, 0, s)
-        quantize_w_passes(1)
-        for s in range(SLICES - 1):
-            nc.scalar.activation(y[0][:, cols(s)], acc[0, s][:], IDENTITY, bias=bias[:, 0:1])
-        nc.vector.tensor_scalar(y[0][:, cols(SLICES - 1)], acc[0, SLICES - 1][:], bias[:, 0:1], None, ADD)
-        for s in range(SLICES):
+        pieces = [(rest, 0, SLICE, SLICE), (rest, SLICE, 2 * SLICE, 2 * SLICE), (first, 0, P, 0), (first, P, SLICE, P)]
+        acc0 = [psum.tile([P, c1 - c0], F32, name=f"acc0{n}") for n, (side, c0, c1, y0) in enumerate(pieces)]
+        quantize(w_codes[0][:, 0], w_scales[0][:, 0], w_bf_first[0][:])
+        for n, (side, c0, c1, y0) in enumerate(pieces):
+            multiply(acc0[n][:], 0, 0, side[0], c0, c1)
+        picked_last = keep.tile([P, 1, SLICE], F32, name="picked_last", tag="w_bf_first0", align_bytes=64)
+        nc.vector.tensor_copy(picked_last[:, 0, :], plane[1, 3][:].indirect(offsets(0, SLICE)))
+        for side, c0, c1, y0 in pieces[2:]:
+            round_slots(x_bf_first[1][:, c0:c1], 3, picked_last[:, :, c0:c1])
+        quantize(w_codes[0][:, 1], w_scales[0][:, 1], w_bf_first[1][:])
+        rest[1] = packed("rest1", S - SLICE, "w_bf_first1")
+        first[1] = packed("first1", SLICE, "first1_codes")
+        for side, c0, c1, y0 in pieces:
+            grouped = x_bf_rest[1] if side is rest else x_bf_first[1]
+            quantize(side[1][0][:, c0:c1], side[1][1][:, c0:c1], grouped[:, c0:c1])
+        for n, (side, c0, c1, y0) in enumerate(pieces):
+            multiply(acc0[n][:], 1, 0, side[1], c0, c1)
+        w_bf_second = keep.tile([P, PASSES, P, PACK], BF16, name="w_bf_second", tag="x_bf_first1", align_bytes=64)
+        for a in range(PASSES):
+            interleave(nc.vector.tensor_copy, w_bf_second[:, a], w_raw[a, 1][:])
+        for a in range(PASSES):
+            quantize(w_codes[1][:, a], w_scales[1][:, a], w_bf_second[:, a])
+        for n, (side, c0, c1, y0) in enumerate(pieces):
+            nc.scalar.activation(y[0][:, y0 : y0 + c1 - c0], acc0[n][:], IDENTITY, bias=bias[:, 0:1])
+        for side, width, y0 in ((rest, S - SLICE, SLICE), (first, SLICE, 0)):
+            acc1 = psum.tile([P, width], F32, name=f"acc1{y0}")
             for a in range(PASSES):
-                multiply(a, 1, s)
-            nc.scalar.activation(y[1][:, cols(s)], acc[1, s][:], IDENTITY, bias=bias[:, 1:2])
+                multiply(acc1[:], a, 1, side[a], 0, width)
+            nc.scalar.activation(y[1][:, y0 : y0 + width], acc1[:], IDENTITY, bias=bias[:, 1:2])
         weighted(0, 0, 0, V)
         weighted(0, 1, 0, V)
         weighted(1, 0, 0, V)

@@ -34,16 +34,11 @@ def tile_picked_sub_lin_bias_sub_e_kernel(tc, xT, w, b, gate, offs, pos1, pos2, 
         offs_sb = keep.tile([P, S // STRIPE], U16, name="offs_sb")
         pos_sb = [keep.tile([P, V // STRIPE], U16, name=f"pos_sb{d}") for d in range(D)]
 
-        warm = keep.tile([P, 8], F32, name="warm")
-        warm_out = keep.tile([P, 8], F32, name="warm_out")
-        nc.gpsimd.memset(warm[:], 0.0)
-        nc.scalar.activation(warm_out[:], warm[:], IDENTITY)
-
         x_rows = xT.rearrange("(a p j) t -> a j p t", p=P, j=PACK)
         order = [(a, j) for a in range(PASSES) for j in range(PACK)]
         plane = {}
         for n, (a, j) in enumerate(order):
-            plane[a, j] = keep.tile([P, T], F32, name=f"plane{a}{j}", align_bytes=64)
+            plane[a, j] = keep.tile([P, T], F32, name=f"plane{a}{j}", align_bytes=256)
             nc.sync.dma_start(plane[a, j][:], x_rows[a, j])
             if n == 0:
                 nc.sync.dma_start(offs_sb[:], offs)
@@ -51,13 +46,13 @@ def tile_picked_sub_lin_bias_sub_e_kernel(tc, xT, w, b, gate, offs, pos1, pos2, 
         w_raw = {}
         for h in range(BLOCKS):
             for a in range(PASSES):
-                w_raw[a, h] = keep.tile([P, PACK, P], F32, name=f"w_raw{a}{h}")
+                w_raw[a, h] = keep.tile([P, PACK, P], F32, name=f"w_raw{a}{h}", align_bytes=256)
                 nc.sync.dma_start(w_raw[a, h][:], w_rows[a][:, :, h * P : (h + 1) * P])
         bias = keep.tile([P, BLOCKS], F32, name="bias")
         with nc.allow_non_contiguous_dma(reason="one bias value a partition and block"):
             nc.sync.dma_start(bias[:], b.rearrange("(h p) o -> p (h o)", p=P))
         nc.sync.dma_start(pos_sb[0][:], pos1)
-        gate_sb = keep.tile([P, D, V], F32, name="gate_sb")
+        gate_sb = keep.tile([P, D, V], F32, name="gate_sb", align_bytes=256)
         nc.sync.dma_start(gate_sb[:], gate[:, :P, :].rearrange("d p v -> p d v"))
         nc.sync.dma_start(pos_sb[1][:], pos2)
 
@@ -79,7 +74,7 @@ def tile_picked_sub_lin_bias_sub_e_kernel(tc, xT, w, b, gate, offs, pos1, pos2, 
         picked[1, 0] = keep.tile([P, 3, S], F32, name="picked10")
         y = [keep.tile([P, S], F32, name=f"y{h}") for h in range(BLOCKS)]
         term = {(h, d): keep.tile([P, V], F32, name=f"term{h}{d}") for h in range(BLOCKS) for d in range(D)}
-        result = [keep.tile([P, V], F32, name=f"result{h}") for h in range(BLOCKS)]
+        result = [keep.tile([P, V], F32, name=f"result{h}", align_bytes=256) for h in range(BLOCKS)]
 
         def interleave(copy, dst, src):
             copy(dst.rearrange("p (c i) t -> p c t i", i=4), src.rearrange("p t (c i) -> p c t i", i=4))
@@ -87,8 +82,8 @@ def tile_picked_sub_lin_bias_sub_e_kernel(tc, xT, w, b, gate, offs, pos1, pos2, 
         def quantize(codes, scales, grouped):
             nc.vector.quantize_mx(out=codes.bitcast(FP8X4), scales=scales, in_=grouped.rearrange("p c t -> p (c t)"))
 
-        def packed(name, width, tag):
-            codes = keep.tile([P, width], U32, name=f"{name}_codes", tag=tag, align_bytes=64)
+        def packed(name, width, tag, align=64):
+            codes = keep.tile([P, width], U32, name=f"{name}_codes", tag=tag, align_bytes=align)
             scales = keep.tile([P, width], U8, name=f"{name}_scales", align_bytes=64)
             return codes, scales
 
@@ -113,7 +108,7 @@ def tile_picked_sub_lin_bias_sub_e_kernel(tc, xT, w, b, gate, offs, pos1, pos2, 
             nc.sync.dma_start(out[h * P : (h + 1) * P, v0:v1], result[h][:, v0:v1])
 
         def round_slots(dst, j0, src):
-            nc.scalar.copy(dst[:, :, j0 : j0 + src.shape[1]], src.rearrange("p t c -> p c t"))
+            nc.scalar.activation(dst[:, :, j0 : j0 + src.shape[1]], src.rearrange("p t c -> p c t"), IDENTITY)
 
         def gather_pair(a, u):
             nc.vector.tensor_copy(picked[a, u][:, 0, :], plane[a, 2 * u][:].indirect(offs_sb[:]))
@@ -129,7 +124,7 @@ def tile_picked_sub_lin_bias_sub_e_kernel(tc, xT, w, b, gate, offs, pos1, pos2, 
         gather_pair(0, 1)
         gather_pair(1, 0)
         first = {0: packed("first0", SLICE, "first0_codes")}
-        rest = {0: packed("rest0", S - SLICE, "plane10")}
+        rest = {0: packed("rest0", S - SLICE, "plane10", 256)}
         quantize(first[0][0][:], first[0][1][:], x_bf_first[0][:])
         quantize(rest[0][0][:], rest[0][1][:], x_bf_rest[0][:])
 

@@ -48,13 +48,14 @@ def tile_picked_sub_lin_bias_sub_e_kernel(tc, xT, w, b, gate, offs, pos1, pos2, 
             for a in range(PASSES):
                 w_raw[a, h] = keep.tile([P, PACK, P], F32, name=f"w_raw{a}{h}", align_bytes=256)
                 nc.sync.dma_start(w_raw[a, h][:], w_rows[a][:, :, h * P : (h + 1) * P])
-        bias = keep.tile([P, BLOCKS], F32, name="bias")
-        with nc.allow_non_contiguous_dma(reason="one bias value a partition and block"):
-            nc.sync.dma_start(bias[:], b.rearrange("(h p) o -> p (h o)", p=P))
+        bias = [keep.tile([P, 1], F32, name=f"bias{h}") for h in range(BLOCKS)]
+        gate_sb = [keep.tile([P, V], F32, name=f"gate_sb{d}", align_bytes=256) for d in range(D)]
+        nc.sync.dma_start(bias[0][:], b[:P])
         nc.sync.dma_start(pos_sb[0][:], pos1)
-        gate_sb = keep.tile([P, D, V], F32, name="gate_sb", align_bytes=256)
-        nc.sync.dma_start(gate_sb[:], gate[:, :P, :].rearrange("d p v -> p d v"))
+        nc.sync.dma_start(gate_sb[0][:], gate[0, :P])
         nc.sync.dma_start(pos_sb[1][:], pos2)
+        nc.sync.dma_start(gate_sb[1][:], gate[1, :P])
+        nc.sync.dma_start(bias[1][:], b[P:])
 
         def offsets(c0, c1):
             return offs_sb[:, c0 // STRIPE : c1 // STRIPE]
@@ -67,14 +68,12 @@ def tile_picked_sub_lin_bias_sub_e_kernel(tc, xT, w, b, gate, offs, pos1, pos2, 
         x_bf = {}
         for a in range(PASSES):
             x_bf[a, 0], x_bf[a, 1], x_bf[a, 2] = x_bf_first[a][:], x_bf_rest[a][:, :SLICE], x_bf_rest[a][:, SLICE:]
-        w_bf_first = [keep.tile([P, P, PACK], BF16, name=f"w_bf_first{a}", align_bytes=64) for a in range(PASSES)]
-        w_codes = [keep.tile([P, PASSES, P], U32, name=f"w_codes{h}", align_bytes=64) for h in range(BLOCKS)]
-        w_scales = [keep.tile([P, PASSES, P], U8, name=f"w_scales{h}", align_bytes=64) for h in range(BLOCKS)]
+        w_bf = {(a, h): keep.tile([P, P, PACK], BF16, name=f"w_bf{a}{h}", align_bytes=64) for a, h in ((0, 0), (1, 0), (0, 1))}
+        w_mx = {}
         picked = {(0, u): keep.tile([P, 2, S], F32, name=f"picked0{u}") for u in range(2)}
         picked[1, 0] = keep.tile([P, 3, S], F32, name="picked10")
         y = [keep.tile([P, S], F32, name=f"y{h}") for h in range(BLOCKS)]
         term = {(h, d): keep.tile([P, V], F32, name=f"term{h}{d}") for h in range(BLOCKS) for d in range(D)}
-        result = [keep.tile([P, V], F32, name=f"result{h}", align_bytes=256) for h in range(BLOCKS)]
 
         def interleave(copy, dst, src):
             copy(dst.rearrange("p (c i) t -> p c t i", i=4), src.rearrange("p t (c i) -> p c t i", i=4))
@@ -91,8 +90,8 @@ def tile_picked_sub_lin_bias_sub_e_kernel(tc, xT, w, b, gate, offs, pos1, pos2, 
             codes, scales = operand
             nc.tensor.matmul_mx(
                 out=acc,
-                lhsT=w_codes[h][:, a].bitcast(FP8X4),
-                lhsT_scale=w_scales[h][:, a],
+                lhsT=w_mx[a, h][0][:].bitcast(FP8X4),
+                lhsT_scale=w_mx[a, h][1][:],
                 rhs=codes[:, c0:c1].bitcast(FP8X4),
                 rhs_scale=scales[:, c0:c1],
                 start=(a == 0),
@@ -101,11 +100,16 @@ def tile_picked_sub_lin_bias_sub_e_kernel(tc, xT, w, b, gate, offs, pos1, pos2, 
 
         def weighted(h, d, v0, v1):
             where = pos_sb[d][:, v0 // STRIPE : v1 // STRIPE]
-            nc.vector.tensor_tensor(term[h, d][:, v0:v1], y[h][:].indirect(where), gate_sb[:, d, v0:v1], MULT)
+            nc.vector.tensor_tensor(term[h, d][:, v0:v1], y[h][:].indirect(where), gate_sb[d][:, v0:v1], MULT)
 
-        def finish(h, v0, v1):
-            nc.vector.tensor_tensor(result[h][:, v0:v1], term[h, 0][:, v0:v1], term[h, 1][:, v0:v1], ADD)
-            nc.sync.dma_start(out[h * P : (h + 1) * P, v0:v1], result[h][:, v0:v1])
+        def finish(h, v0, v1, tag):
+            result = keep.tile([P, v1 - v0], F32, name=f"result{h}{v0}", tag=tag, align_bytes=256)
+            nc.vector.tensor_tensor(result[:], term[h, 0][:, v0:v1], term[h, 1][:, v0:v1], ADD)
+            nc.sync.dma_start(out[h * P : (h + 1) * P, v0:v1], result[:])
+
+        def quantize_w(a, h, tag):
+            w_mx[a, h] = packed(f"w{a}{h}", P, tag)
+            quantize(w_mx[a, h][0][:], w_mx[a, h][1][:], w_bf[a, h][:])
 
         def round_slots(dst, j0, src):
             nc.scalar.activation(dst[:, :, j0 : j0 + src.shape[1]], src.rearrange("p t c -> p c t"), IDENTITY)
@@ -132,43 +136,44 @@ def tile_picked_sub_lin_bias_sub_e_kernel(tc, xT, w, b, gate, offs, pos1, pos2, 
         round_slots(x_bf[1, 0], 0, picked[1, 0][:, :, cols(0)])
         gather_rest(2)
         gather_rest(3)
-        for a in range(PASSES):
-            interleave(nc.scalar.copy, w_bf_first[a][:], w_raw[a, 0][:])
+        for a, h in ((0, 0), (1, 0), (0, 1)):
+            interleave(nc.scalar.copy, w_bf[a, h][:], w_raw[a, h][:])
 
         pieces = [(rest, 0, SLICE, SLICE), (rest, SLICE, 2 * SLICE, 2 * SLICE), (first, 0, P, 0), (first, P, SLICE, P)]
         acc0 = [psum.tile([P, c1 - c0], F32, name=f"acc0{n}") for n, (side, c0, c1, y0) in enumerate(pieces)]
-        quantize(w_codes[0][:, 0], w_scales[0][:, 0], w_bf_first[0][:])
+        quantize_w(0, 0, "w00_codes")
         for n, (side, c0, c1, y0) in enumerate(pieces):
             multiply(acc0[n][:], 0, 0, side[0], c0, c1)
-        picked_last = keep.tile([P, 1, SLICE], F32, name="picked_last", tag="w_bf_first0", align_bytes=64)
+        picked_last = keep.tile([P, 1, SLICE], F32, name="picked_last", tag="w_bf00", align_bytes=64)
         nc.vector.tensor_copy(picked_last[:, 0, :], plane[1, 3][:].indirect(offsets(0, SLICE)))
         for side, c0, c1, y0 in pieces[2:]:
             round_slots(x_bf_first[1][:, c0:c1], 3, picked_last[:, :, c0:c1])
-        quantize(w_codes[0][:, 1], w_scales[0][:, 1], w_bf_first[1][:])
-        rest[1] = packed("rest1", S - SLICE, "w_bf_first1")
+        quantize_w(1, 0, "w10_codes")
+        rest[1] = packed("rest1", S - SLICE, "w_bf10")
         first[1] = packed("first1", SLICE, "first1_codes")
         for side, c0, c1, y0 in pieces:
             grouped = x_bf_rest[1] if side is rest else x_bf_first[1]
             quantize(side[1][0][:, c0:c1], side[1][1][:, c0:c1], grouped[:, c0:c1])
         for n, (side, c0, c1, y0) in enumerate(pieces):
             multiply(acc0[n][:], 1, 0, side[1], c0, c1)
-        w_bf_second = keep.tile([P, PASSES, P, PACK], BF16, name="w_bf_second", tag="x_bf_first1", align_bytes=64)
-        for a in range(PASSES):
-            interleave(nc.vector.tensor_copy, w_bf_second[:, a], w_raw[a, 1][:])
-        for a in range(PASSES):
-            quantize(w_codes[1][:, a], w_scales[1][:, a], w_bf_second[:, a])
+        quantize_w(0, 1, "x_bf_first1")
+        w_bf[1, 1] = keep.tile([P, P, PACK], BF16, name="w_bf11", tag="w_bf01", align_bytes=64)
+        interleave(nc.vector.tensor_copy, w_bf[1, 1][:], w_raw[1, 1][:])
+        quantize_w(1, 1, "w11_codes")
         for n, (side, c0, c1, y0) in enumerate(pieces):
-            nc.scalar.activation(y[0][:, y0 : y0 + c1 - c0], acc0[n][:], IDENTITY, bias=bias[:, 0:1])
-        for side, width, y0 in ((rest, S - SLICE, SLICE), (first, SLICE, 0)):
-            acc1 = psum.tile([P, width], F32, name=f"acc1{y0}")
-            for a in range(PASSES):
-                multiply(acc1[:], a, 1, side[a], 0, width)
-            nc.scalar.activation(y[1][:, y0 : y0 + width], acc1[:], IDENTITY, bias=bias[:, 1:2])
+            nc.scalar.activation(y[0][:, y0 : y0 + c1 - c0], acc0[n][:], IDENTITY, bias=bias[0][:])
+        thirds = pieces[:2] + [(first, 0, SLICE, 0)]
+        acc1 = [psum.tile([P, SLICE], F32, name=f"acc1{n}") for n in range(SLICES)]
+        for a in range(PASSES):
+            for n, (side, c0, c1, y0) in enumerate(thirds):
+                multiply(acc1[n][:], a, 1, side[a], c0, c1)
+        for n, (side, c0, c1, y0) in enumerate(thirds):
+            nc.scalar.activation(y[1][:, y0 : y0 + SLICE], acc1[n][:], IDENTITY, bias=bias[1][:])
         weighted(0, 0, 0, V)
         weighted(0, 1, 0, V)
         weighted(1, 0, 0, V)
-        finish(0, 0, V)
+        finish(0, 0, V, "gate_sb0")
         weighted(1, 1, 0, 256)
         weighted(1, 1, 256, V)
-        finish(1, 0, 256)
-        finish(1, 256, V)
+        finish(1, 0, 256, "result_wide")
+        finish(1, 256, V, "result_last")

@@ -1,6 +1,7 @@
 from contextlib import ExitStack
 
 import concourse.mybir as mybir
+from concourse.masks import make_identity
 
 K, T, D, S, V, N = 1024, 2048, 2, 768, 384, 256
 FLOPS = 2 * K * N * S
@@ -57,17 +58,21 @@ def tile_picked_sub_lin_bias_sub_e_kernel(tc, xT, w, b, gate, offs, pos1, pos2, 
         nc.sync.dma_start(gate_sb[1][:], gate[1, :P])
         nc.sync.dma_start(bias[1][:], b[P:])
 
+        identity = keep.tile([P, P], F32, name="identity")
+        make_identity(nc, identity[:])
+
         def offsets(c0, c1):
             return offs_sb[:, c0 // STRIPE : c1 // STRIPE]
 
         def cols(s):
             return slice(s * SLICE, (s + 1) * SLICE)
 
-        x_bf_first = [keep.tile([P, SLICE, PACK], BF16, name=f"x_bf_first{a}", align_bytes=64) for a in range(PASSES)]
+        x_bf_first = [keep.tile([P, SLICE, PACK], BF16, name="x_bf_first0", align_bytes=64)]
         x_bf_rest = [keep.tile([P, S - SLICE, PACK], BF16, name=f"x_bf_rest{a}", align_bytes=64) for a in range(PASSES)]
         x_bf = {}
         for a in range(PASSES):
-            x_bf[a, 0], x_bf[a, 1], x_bf[a, 2] = x_bf_first[a][:], x_bf_rest[a][:, :SLICE], x_bf_rest[a][:, SLICE:]
+            x_bf[a, 1], x_bf[a, 2] = x_bf_rest[a][:, :SLICE], x_bf_rest[a][:, SLICE:]
+        x_bf[0, 0] = x_bf_first[0][:]
         w_bf = {(a, h): keep.tile([P, P, PACK], BF16, name=f"w_bf{a}{h}", align_bytes=64) for a, h in ((0, 0), (1, 0), (0, 1))}
         w_mx = {}
         picked = {(0, u): keep.tile([P, 2, S], F32, name=f"picked0{u}") for u in range(2)}
@@ -107,8 +112,8 @@ def tile_picked_sub_lin_bias_sub_e_kernel(tc, xT, w, b, gate, offs, pos1, pos2, 
             nc.vector.tensor_tensor(result[:], term[h, 0][:, v0:v1], term[h, 1][:, v0:v1], ADD)
             nc.sync.dma_start(out[h * P : (h + 1) * P, v0:v1], result[:])
 
-        def quantize_w(a, h, tag):
-            w_mx[a, h] = packed(f"w{a}{h}", P, tag)
+        def quantize_w(a, h, tag, align=64):
+            w_mx[a, h] = packed(f"w{a}{h}", P, tag, align)
             quantize(w_mx[a, h][0][:], w_mx[a, h][1][:], w_bf[a, h][:])
 
         def round_slots(dst, j0, src):
@@ -133,7 +138,9 @@ def tile_picked_sub_lin_bias_sub_e_kernel(tc, xT, w, b, gate, offs, pos1, pos2, 
         quantize(rest[0][0][:], rest[0][1][:], x_bf_rest[0][:])
 
         nc.vector.tensor_copy(picked[1, 0][:, 2, cols(0)], plane[1, 2][:].indirect(offsets(0, SLICE)))
-        round_slots(x_bf[1, 0], 0, picked[1, 0][:, :, cols(0)])
+        x_bf_halves = [keep.tile([P, P, PACK], BF16, name=f"x_bf_half{n}", align_bytes=64) for n in range(2)]
+        for n in range(2):
+            round_slots(x_bf_halves[n][:], 0, picked[1, 0][:, :, n * P : (n + 1) * P])
         gather_rest(2)
         gather_rest(3)
         for a, h in ((0, 0), (1, 0), (0, 1)):
@@ -144,35 +151,49 @@ def tile_picked_sub_lin_bias_sub_e_kernel(tc, xT, w, b, gate, offs, pos1, pos2, 
         quantize_w(0, 0, "w00_codes")
         for n, (side, c0, c1, y0) in enumerate(pieces):
             multiply(acc0[n][:], 0, 0, side[0], c0, c1)
-        picked_last = keep.tile([P, 1, SLICE], F32, name="picked_last", tag="w_bf00", align_bytes=64)
+        picked_last = keep.tile([P, 1, SLICE], F32, name="picked_last", tag="w_raw00", align_bytes=256)
         nc.vector.tensor_copy(picked_last[:, 0, :], plane[1, 3][:].indirect(offsets(0, SLICE)))
-        for side, c0, c1, y0 in pieces[2:]:
-            round_slots(x_bf_first[1][:, c0:c1], 3, picked_last[:, :, c0:c1])
+        for n in range(2):
+            round_slots(x_bf_halves[n][:], 3, picked_last[:, :, n * P : (n + 1) * P])
         quantize_w(1, 0, "w10_codes")
-        rest[1] = packed("rest1", S - SLICE, "w_bf10")
+        rest[1] = packed("rest1", S - SLICE, "w_raw10", 256)
         first[1] = packed("first1", SLICE, "first1_codes")
         for side, c0, c1, y0 in pieces:
-            grouped = x_bf_rest[1] if side is rest else x_bf_first[1]
-            quantize(side[1][0][:, c0:c1], side[1][1][:, c0:c1], grouped[:, c0:c1])
+            grouped = x_bf_rest[1][:, c0:c1] if side is rest else x_bf_halves[c0 // P][:]
+            quantize(side[1][0][:, c0:c1], side[1][1][:, c0:c1], grouped)
         for n, (side, c0, c1, y0) in enumerate(pieces):
             multiply(acc0[n][:], 1, 0, side[1], c0, c1)
-        quantize_w(0, 1, "x_bf_first1")
-        w_bf[1, 1] = keep.tile([P, P, PACK], BF16, name="w_bf11", tag="w_bf01", align_bytes=64)
+        quantize_w(0, 1, "w_raw00", 256)
+        w_bf[1, 1] = keep.tile([P, P, PACK], BF16, name="w_bf11", tag="x_bf_half1", align_bytes=64)
         interleave(nc.vector.tensor_copy, w_bf[1, 1][:], w_raw[1, 1][:])
         quantize_w(1, 1, "w11_codes")
         for n, (side, c0, c1, y0) in enumerate(pieces):
             nc.scalar.activation(y[0][:, y0 : y0 + c1 - c0], acc0[n][:], IDENTITY, bias=bias[0][:])
-        thirds = pieces[:2] + [(first, 0, SLICE, 0)]
-        acc1 = [psum.tile([P, SLICE], F32, name=f"acc1{n}") for n in range(SLICES)]
+        acc1 = [psum.tile([P, c1 - c0], F32, name=f"acc1{n}", tag=f"acc0{n}") for n, (side, c0, c1, y0) in enumerate(pieces)]
         for a in range(PASSES):
-            for n, (side, c0, c1, y0) in enumerate(thirds):
+            for n, (side, c0, c1, y0) in enumerate(pieces):
                 multiply(acc1[n][:], a, 1, side[a], c0, c1)
-        for n, (side, c0, c1, y0) in enumerate(thirds):
-            nc.scalar.activation(y[1][:, y0 : y0 + SLICE], acc1[n][:], IDENTITY, bias=bias[1][:])
+        for n, (side, c0, c1, y0) in enumerate(pieces):
+            nc.scalar.activation(y[1][:, y0 : y0 + c1 - c0], acc1[n][:], IDENTITY, bias=bias[1][:])
         weighted(0, 0, 0, V)
-        weighted(0, 1, 0, V)
+        weighted(0, 1, 0, 256)
+        weighted(0, 1, 256, V)
         weighted(1, 0, 0, V)
-        finish(0, 0, V, "gate_sb0")
+        turned = keep.tile([P, 3, P], F32, name="turned", tag="bias1")
+        summed = keep.tile([P, 3, P], F32, name="summed", align_bytes=256)
+        sums = [psum.tile([P, P], F32, name=f"sums{c}") for c in range(2)] + [psum.tile([P, P], F32, name="sums2", tag="acc00")]
+        backs = [psum.tile([P, P], F32, name=f"backs{c}") for c in range(2)] + [psum.tile([P, P], F32, name="backs2", tag="acc01")]
+        for d in range(D):
+            for c in range(3):
+                nc.tensor.matmul(sums[c][:], term[0, d][:, c * P : (c + 1) * P], identity[:], start=(d == 0), stop=(d == D - 1), is_transpose=True)
+        for c in range(3):
+            nc.scalar.copy(turned[:, c], sums[c][:])
+        for c in range(3):
+            nc.tensor.transpose(backs[c][:], turned[:, c], identity[:])
+        for c in range(3):
+            nc.scalar.copy(summed[:, c], backs[c][:])
+        nc.scalar.dma_start(out[:P, : 2 * P], summed[:, :2].rearrange("p c v -> p (c v)"))
+        nc.scalar.dma_start(out[:P, 2 * P :], summed[:, 2])
         weighted(1, 1, 0, 256)
         weighted(1, 1, 256, V)
         finish(1, 0, 256, "result_wide")

@@ -119,19 +119,20 @@ def tile_picked_sub_lin_bias_sub_e_kernel(tc, xT, w, b, gate, offs, pos1, pos2, 
         def round_slots(dst, j0, src):
             nc.scalar.activation(dst[:, :, j0 : j0 + src.shape[1]], src.rearrange("p t c -> p c t"), IDENTITY)
 
-        def gather_pair(a, u):
+        def gather_pair(a, u, cuts):
             nc.vector.tensor_copy(picked[a, u][:, 0, :], plane[a, 2 * u][:].indirect(offs_sb[:]))
-            for s in range(SLICES):
-                nc.vector.tensor_copy(picked[a, u][:, 1, cols(s)], plane[a, 2 * u + 1][:].indirect(offsets(s * SLICE, (s + 1) * SLICE)))
-                if (a, s) != (1, 0):
-                    round_slots(x_bf[a, s], 2 * u, picked[a, u][:, :2, cols(s)])
+            for s0, s1 in zip(cuts, cuts[1:]):
+                nc.vector.tensor_copy(picked[a, u][:, 1, s0 * SLICE : s1 * SLICE], plane[a, 2 * u + 1][:].indirect(offsets(s0 * SLICE, s1 * SLICE)))
+                for s in range(s0, s1):
+                    if (a, s) != (1, 0):
+                        round_slots(x_bf[a, s], 2 * u, picked[a, u][:, :2, cols(s)])
 
         def gather_rest(j):
             nc.vector.tensor_copy(x_bf_rest[1][:, :, j], plane[1, j][:].indirect(offsets(SLICE, S)))
 
-        gather_pair(0, 0)
-        gather_pair(0, 1)
-        gather_pair(1, 0)
+        gather_pair(0, 0, (0, 3))
+        gather_pair(0, 1, (0, 1, 3))
+        gather_pair(1, 0, (0, 2, 3))
         first = {0: packed("first0", SLICE, "first0_codes")}
         rest = {0: packed("rest0", S - SLICE, "plane10", 256)}
         quantize(first[0][0][:], first[0][1][:], x_bf_first[0][:])

@@ -30,6 +30,7 @@ def tile_picked_sub_lin_bias_sub_e_kernel(tc, xT, w, b, gate, offs, pos1, pos2, 
     nc = tc.nc
     with ExitStack() as ctx:
         keep = ctx.enter_context(tc.tile_pool(name="keep", bufs=1))
+        reused = ctx.enter_context(tc.tile_pool(name="reused", bufs=1))
         psum = ctx.enter_context(tc.psum_pool(name="psum", bufs=1))
 
         offs_sb = keep.tile([P, S // STRIPE], U16, name="offs_sb")
@@ -47,7 +48,10 @@ def tile_picked_sub_lin_bias_sub_e_kernel(tc, xT, w, b, gate, offs, pos1, pos2, 
         w_raw = {}
         for h in range(BLOCKS):
             for a in range(PASSES):
-                w_raw[a, h] = keep.tile([P, PACK, P], F32, name=f"w_raw{a}{h}", align_bytes=256)
+                if (a, h) == (0, 0):
+                    w_raw[a, h] = reused.tile([P, PACK, P], F32, name="w_raw00", align_bytes=256, offset=0)
+                else:
+                    w_raw[a, h] = keep.tile([P, PACK, P], F32, name=f"w_raw{a}{h}", align_bytes=256)
                 nc.sync.dma_start(w_raw[a, h][:], w_rows[a][:, :, h * P : (h + 1) * P])
         bias = [keep.tile([P, 1], F32, name=f"bias{h}") for h in range(BLOCKS)]
         gate_sb = [keep.tile([P, V], F32, name=f"gate_sb{d}", align_bytes=256) for d in range(D)]
@@ -149,13 +153,16 @@ def tile_picked_sub_lin_bias_sub_e_kernel(tc, xT, w, b, gate, offs, pos1, pos2, 
 
         pieces = [(rest, 0, SLICE, SLICE), (rest, SLICE, 2 * SLICE, 2 * SLICE), (first, 0, P, 0), (first, P, SLICE, P)]
         acc0 = [psum.tile([P, c1 - c0], F32, name=f"acc0{n}") for n, (side, c0, c1, y0) in enumerate(pieces)]
+        picked_last = reused.tile([P, 1, SLICE], BF16, name="picked_last", align_bytes=256, offset=256)
         quantize_w(0, 0, "w00_codes")
         for n, (side, c0, c1, y0) in enumerate(pieces):
             multiply(acc0[n][:], 0, 0, side[0], c0, c1)
-        picked_last = keep.tile([P, 1, SLICE], F32, name="picked_last", tag="w_raw00", align_bytes=256)
         nc.vector.tensor_copy(picked_last[:, 0, :], plane[1, 3][:].indirect(offsets(0, SLICE)))
         for n in range(2):
             round_slots(x_bf_halves[n][:], 3, picked_last[:, :, n * P : (n + 1) * P])
+        half = P // 2
+        w_bf_last = [keep.tile([P, half, PACK], BF16, name="w_bf_last0", tag="plane13", align_bytes=256)]
+        interleave(nc.scalar.copy, w_bf_last[0][:], w_raw[1, 1][:, :, :half])
         quantize_w(1, 0, "w10_codes")
         rest[1] = packed("rest1", S - SLICE, "w_raw10", 256)
         first[1] = packed("first1", SLICE, "first1_codes")
@@ -164,12 +171,18 @@ def tile_picked_sub_lin_bias_sub_e_kernel(tc, xT, w, b, gate, offs, pos1, pos2, 
             quantize(side[1][0][:, c0:c1], side[1][1][:, c0:c1], grouped)
         for n, (side, c0, c1, y0) in enumerate(pieces):
             multiply(acc0[n][:], 1, 0, side[1], c0, c1)
-        quantize_w(0, 1, "w_raw00", 256)
-        w_bf[1, 1] = keep.tile([P, P, PACK], BF16, name="w_bf11", tag="x_bf_half1", align_bytes=64)
-        interleave(nc.vector.tensor_copy, w_bf[1, 1][:], w_raw[1, 1][:])
-        quantize_w(1, 1, "w11_codes")
+        w_bf_last.append(reused.tile([P, half, PACK], BF16, name="w_bf_last1", align_bytes=256, offset=0))
+        interleave(nc.vector.tensor_copy, w_bf_last[1][:], w_raw[1, 1][:, :, half:])
+        w_mx[0, 1] = (reused.tile([P, P], U32, name="w01_codes", align_bytes=256, offset=512), keep.tile([P, P], U8, name="w01_scales", align_bytes=64))
+        quantize(w_mx[0, 1][0][:], w_mx[0, 1][1][:], w_bf[0, 1][:])
+        w_mx[1, 1] = packed("w11", P, "x_bf_half1")
+        for n in range(2):
+            quantize(w_mx[1, 1][0][:, n * half : (n + 1) * half], w_mx[1, 1][1][:, n * half : (n + 1) * half], w_bf_last[n][:])
         for n, (side, c0, c1, y0) in enumerate(pieces):
-            nc.scalar.activation(y[0][:, y0 : y0 + c1 - c0], acc0[n][:], IDENTITY, bias=bias[0][:])
+            if n == 2:
+                nc.vector.tensor_scalar_add(y[0][:, y0 : y0 + c1 - c0], acc0[n][:], bias[0][:])
+            else:
+                nc.scalar.activation(y[0][:, y0 : y0 + c1 - c0], acc0[n][:], IDENTITY, bias=bias[0][:])
         acc1 = [psum.tile([P, c1 - c0], F32, name=f"acc1{n}", tag=f"acc0{n}") for n, (side, c0, c1, y0) in enumerate(pieces)]
         for a in range(PASSES):
             for n, (side, c0, c1, y0) in enumerate(pieces):

@@ -1,7 +1,6 @@
 from contextlib import ExitStack
 
 import concourse.mybir as mybir
-from concourse.masks import make_identity
 
 K, T, D, S, V, N = 1024, 2048, 2, 768, 384, 256
 FLOPS = 2 * K * N * S
@@ -13,6 +12,7 @@ U16 = mybir.dt.uint16
 U8 = mybir.dt.uint8
 FP8X4 = mybir.dt.float8_e4m3fn_x4
 IDENTITY = mybir.ActivationFunctionType.Identity
+COPY = mybir.ActivationFunctionType.Copy
 ADD = mybir.AluOpType.add
 MULT = mybir.AluOpType.mult
 
@@ -20,41 +20,42 @@ P = 128
 PACK = 4
 K_PASS = P * PACK
 PASSES = K // K_PASS
-SLICE = 256
-SLICES = S // SLICE
 BLOCKS = N // P
 STRIPE = 16
+STEPPED = 512
+DENSE = S - STEPPED
+WIDE = 256
 
 
 def tile_picked_sub_lin_bias_sub_e_kernel(tc, xT, w, b, gate, offs, pos1, pos2, out):
     nc = tc.nc
     with ExitStack() as ctx:
         keep = ctx.enter_context(tc.tile_pool(name="keep", bufs=1))
-        reused = ctx.enter_context(tc.tile_pool(name="reused", bufs=1))
         psum = ctx.enter_context(tc.psum_pool(name="psum", bufs=1))
+
+        def tile(name, shape, dtype, tag=None):
+            return keep.tile(shape, dtype, name=name, tag=tag or name, align_bytes=256)
 
         offs_sb = keep.tile([P, S // STRIPE], U16, name="offs_sb")
         pos_sb = [keep.tile([P, V // STRIPE], U16, name=f"pos_sb{d}") for d in range(D)]
 
-        x_rows = xT.rearrange("(a p j) t -> a j p t", p=P, j=PACK)
-        order = [(a, j) for a in range(PASSES) for j in range(PACK)]
+        x_rows = xT.rearrange("(a p j) t -> a p j t", p=P, j=PACK)
         plane = {}
-        for n, (a, j) in enumerate(order):
-            plane[a, j] = keep.tile([P, T], F32, name=f"plane{a}{j}", align_bytes=256)
-            nc.sync.dma_start(plane[a, j][:], x_rows[a, j])
-            if n == 0:
+        for a, j0, j1 in ((0, 0, 2), (0, 2, 4), (1, 0, 2), (1, 2, 3), (1, 3, 4)):
+            loaded = tile(f"planes{a}{j0}", [P, (j1 - j0) * T], F32)
+            nc.sync.dma_start(loaded[:], x_rows[a][:, j0:j1].rearrange("p j t -> p (j t)"))
+            for j in range(j0, j1):
+                plane[a, j] = loaded[:, (j - j0) * T : (j - j0 + 1) * T]
+            if (a, j0) == (0, 0):
                 nc.sync.dma_start(offs_sb[:], offs)
         w_rows = w.rearrange("(a p j) n -> a p j n", p=P, j=PACK)
         w_raw = {}
         for h in range(BLOCKS):
             for a in range(PASSES):
-                if (a, h) == (0, 0):
-                    w_raw[a, h] = reused.tile([P, PACK, P], F32, name="w_raw00", align_bytes=256, offset=0)
-                else:
-                    w_raw[a, h] = keep.tile([P, PACK, P], F32, name=f"w_raw{a}{h}", align_bytes=256)
+                w_raw[a, h] = tile(f"w_raw{a}{h}", [P, PACK, P], F32)
                 nc.sync.dma_start(w_raw[a, h][:], w_rows[a][:, :, h * P : (h + 1) * P])
-        bias = [keep.tile([P, 1], F32, name=f"bias{h}") for h in range(BLOCKS)]
-        gate_sb = [keep.tile([P, V], F32, name=f"gate_sb{d}", align_bytes=256) for d in range(D)]
+        bias = [tile(f"bias{h}", [P, 1], F32) for h in range(BLOCKS)]
+        gate_sb = [tile(f"gate_sb{d}", [P, V], F32) for d in range(D)]
         nc.sync.dma_start(bias[0][:], b[:P])
         nc.sync.dma_start(pos_sb[0][:], pos1)
         nc.sync.dma_start(gate_sb[0][:], gate[0, :P])
@@ -62,41 +63,43 @@ def tile_picked_sub_lin_bias_sub_e_kernel(tc, xT, w, b, gate, offs, pos1, pos2, 
         nc.sync.dma_start(gate_sb[1][:], gate[1, :P])
         nc.sync.dma_start(bias[1][:], b[P:])
 
-        identity = keep.tile([P, P], F32, name="identity")
-        make_identity(nc, identity[:])
-
         def offsets(c0, c1):
             return offs_sb[:, c0 // STRIPE : c1 // STRIPE]
 
-        def cols(s):
-            return slice(s * SLICE, (s + 1) * SLICE)
+        def vector_gather(dst, window, where):
+            nc.vector.tensor_copy(dst, window.indirect(where))
 
-        x_bf_first = [keep.tile([P, SLICE, PACK], BF16, name="x_bf_first0", align_bytes=64)]
-        x_bf_rest = [keep.tile([P, S - SLICE, PACK], BF16, name=f"x_bf_rest{a}", align_bytes=64) for a in range(PASSES)]
-        x_bf = {}
-        for a in range(PASSES):
-            x_bf[a, 1], x_bf[a, 2] = x_bf_rest[a][:, :SLICE], x_bf_rest[a][:, SLICE:]
-        x_bf[0, 0] = x_bf_first[0][:]
-        w_bf = {(a, h): keep.tile([P, P, PACK], BF16, name=f"w_bf{a}{h}", align_bytes=64) for a, h in ((0, 0), (1, 0), (0, 1))}
-        w_mx = {}
-        picked = {(0, u): keep.tile([P, 2, S], F32, name=f"picked0{u}") for u in range(2)}
-        picked[1, 0] = keep.tile([P, 3, S], F32, name="picked10")
-        y = [keep.tile([P, S], F32, name=f"y{h}") for h in range(BLOCKS)]
-        term = {(h, d): keep.tile([P, V], F32, name=f"term{h}{d}") for h in range(BLOCKS) for d in range(D)}
+        def scalar_gather(dst, window, where):
+            nc.scalar.activation(dst, window.indirect(where), COPY)
 
-        def interleave(copy, dst, src):
+        def scalar_round(dst, src):
+            nc.scalar.activation(dst, src, IDENTITY)
+
+        def weave(copy, dst, src):
             copy(dst.rearrange("p (c i) t -> p c t i", i=4), src.rearrange("p t (c i) -> p c t i", i=4))
 
-        def quantize(codes, scales, grouped):
-            nc.vector.quantize_mx(out=codes.bitcast(FP8X4), scales=scales, in_=grouped.rearrange("p c t -> p (c t)"))
+        def weave_pair(copy, dst, j0, src):
+            copy(dst[:, :, j0 : j0 + 2], src.rearrange("p t c -> p c t"))
 
-        def packed(name, width, tag, align=64):
-            codes = keep.tile([P, width], U32, name=f"{name}_codes", tag=tag, align_bytes=align)
-            scales = keep.tile([P, width], U8, name=f"{name}_scales", align_bytes=64)
-            return codes, scales
-
-        def multiply(acc, a, h, operand, c0, c1):
+        def quantize(operand, c0, c1, grouped):
             codes, scales = operand
+            nc.vector.quantize_mx(out=codes[:, c0:c1].bitcast(FP8X4), scales=scales[:, c0:c1], in_=grouped.rearrange("p c t -> p (c t)"))
+
+        def packed(name, width, tag=None):
+            return tile(f"{name}_codes", [P, width], U32, tag), tile(f"{name}_scales", [P, width], U8)
+
+        w_bf, w_mx, x_mx = {}, {}, {}
+
+        def round_w(copy, a, h):
+            w_bf[a, h] = tile(f"w_bf{a}{h}", [P, P, PACK], BF16)
+            weave(copy, w_bf[a, h][:], w_raw[a, h][:])
+
+        def quantize_w(a, h, tag=None):
+            w_mx[a, h] = packed(f"w{a}{h}", P, tag)
+            quantize(w_mx[a, h], 0, P, w_bf[a, h][:])
+
+        def multiply(acc, a, h, c0, c1):
+            codes, scales = x_mx[a]
             nc.tensor.matmul_mx(
                 out=acc,
                 lhsT=w_mx[a, h][0][:].bitcast(FP8X4),
@@ -107,108 +110,86 @@ def tile_picked_sub_lin_bias_sub_e_kernel(tc, xT, w, b, gate, offs, pos1, pos2, 
                 stop=(a == PASSES - 1),
             )
 
-        def weighted(h, d, v0, v1):
-            where = pos_sb[d][:, v0 // STRIPE : v1 // STRIPE]
-            nc.vector.tensor_tensor(term[h, d][:, v0:v1], y[h][:].indirect(where), gate_sb[d][:, v0:v1], MULT)
+        picked0 = tile("picked0", [P, PACK, S], F32)
+        x_bf0 = [tile("x_bf0_first", [P, WIDE, PACK], BF16), tile("x_bf0_rest", [P, S - WIDE, PACK], BF16)]
+        for j in range(3):
+            vector_gather(picked0[:, j], plane[0, j], offs_sb[:])
+        weave_pair(scalar_round, x_bf0[0][:], 0, picked0[:, :2, :WIDE])
+        scalar_gather(picked0[:, 3], plane[0, 3], offs_sb[:])
+        weave_pair(scalar_round, x_bf0[0][:], 2, picked0[:, 2:, :WIDE])
+        weave(nc.vector.tensor_copy, x_bf0[1][:], picked0[:, :, WIDE:])
+        x_mx[0] = packed("x0", S)
+        quantize(x_mx[0], 0, WIDE, x_bf0[0][:])
+        quantize(x_mx[0], WIDE, S, x_bf0[1][:])
 
-        def finish(h, v0, v1, tag):
-            result = keep.tile([P, v1 - v0], F32, name=f"result{h}{v0}", tag=tag, align_bytes=256)
-            nc.vector.tensor_tensor(result[:], term[h, 0][:, v0:v1], term[h, 1][:, v0:v1], ADD)
-            nc.sync.dma_start(out[h * P : (h + 1) * P, v0:v1], result[:])
+        stepped = tile("x_bf1_stepped", [P, STEPPED, PACK], BF16)
+        dense = tile("x_bf1_dense", [P, PACK, DENSE], BF16)
+        picked1 = [tile("picked1_stepped", [P, 2, STEPPED], F32), tile("picked1_dense", [P, 2, DENSE], F32)]
+        vector_gather(picked1[0][:, 0], plane[1, 0], offsets(0, STEPPED))
+        scalar_gather(picked1[0][:, 1], plane[1, 1], offsets(0, STEPPED))
+        weave_pair(nc.vector.tensor_copy, stepped[:], 0, picked1[0][:])
+        for j in range(2):
+            scalar_gather(picked1[1][:, j], plane[1, j], offsets(STEPPED, S))
+        nc.scalar.copy(dense[:, :2], picked1[1][:])
+        for j in (2, 3):
+            vector_gather(stepped[:, :, j], plane[1, j], offsets(0, STEPPED))
+            scalar_gather(dense[:, j], plane[1, j], offsets(STEPPED, S))
+        for a, h in ((0, 0), (1, 0), (0, 1), (1, 1)):
+            round_w(nc.scalar.copy, a, h)
 
-        def quantize_w(a, h, tag, align=64):
-            w_mx[a, h] = packed(f"w{a}{h}", P, tag, align)
-            quantize(w_mx[a, h][0][:], w_mx[a, h][1][:], w_bf[a, h][:])
-
-        def round_slots(dst, j0, src):
-            nc.scalar.activation(dst[:, :, j0 : j0 + src.shape[1]], src.rearrange("p t c -> p c t"), IDENTITY)
-
-        def gather_pair(a, u, cuts):
-            nc.vector.tensor_copy(picked[a, u][:, 0, :], plane[a, 2 * u][:].indirect(offs_sb[:]))
-            for s0, s1 in zip(cuts, cuts[1:]):
-                nc.vector.tensor_copy(picked[a, u][:, 1, s0 * SLICE : s1 * SLICE], plane[a, 2 * u + 1][:].indirect(offsets(s0 * SLICE, s1 * SLICE)))
-                for s in range(s0, s1):
-                    if (a, s) != (1, 0):
-                        round_slots(x_bf[a, s], 2 * u, picked[a, u][:, :2, cols(s)])
-
-        def gather_rest(j):
-            nc.vector.tensor_copy(x_bf_rest[1][:, :, j], plane[1, j][:].indirect(offsets(SLICE, S)))
-
-        gather_pair(0, 0, (0, 3))
-        gather_pair(0, 1, (0, 1, 3))
-        gather_pair(1, 0, (0, 2, 3))
-        first = {0: packed("first0", SLICE, "first0_codes")}
-        rest = {0: packed("rest0", S - SLICE, "plane10", 256)}
-        quantize(first[0][0][:], first[0][1][:], x_bf_first[0][:])
-        quantize(rest[0][0][:], rest[0][1][:], x_bf_rest[0][:])
-
-        nc.vector.tensor_copy(picked[1, 0][:, 2, cols(0)], plane[1, 2][:].indirect(offsets(0, SLICE)))
-        x_bf_halves = [keep.tile([P, P, PACK], BF16, name=f"x_bf_half{n}", align_bytes=64) for n in range(2)]
-        for n in range(2):
-            round_slots(x_bf_halves[n][:], 0, picked[1, 0][:, :, n * P : (n + 1) * P])
-        gather_rest(2)
-        gather_rest(3)
-        for a, h in ((0, 0), (1, 0), (0, 1)):
-            interleave(nc.scalar.copy, w_bf[a, h][:], w_raw[a, h][:])
-
-        pieces = [(rest, 0, SLICE, SLICE), (rest, SLICE, 2 * SLICE, 2 * SLICE), (first, 0, P, 0), (first, P, SLICE, P)]
-        acc0 = [psum.tile([P, c1 - c0], F32, name=f"acc0{n}") for n, (side, c0, c1, y0) in enumerate(pieces)]
-        picked_last = reused.tile([P, 1, SLICE], BF16, name="picked_last", align_bytes=256, offset=256)
-        quantize_w(0, 0, "w00_codes")
-        for n, (side, c0, c1, y0) in enumerate(pieces):
-            multiply(acc0[n][:], 0, 0, side[0], c0, c1)
-        nc.vector.tensor_copy(picked_last[:, 0, :], plane[1, 3][:].indirect(offsets(0, SLICE)))
-        for n in range(2):
-            round_slots(x_bf_halves[n][:], 3, picked_last[:, :, n * P : (n + 1) * P])
-        half = P // 2
-        w_bf_last = [keep.tile([P, half, PACK], BF16, name="w_bf_last0", tag="plane13", align_bytes=256)]
-        interleave(nc.scalar.copy, w_bf_last[0][:], w_raw[1, 1][:, :, :half])
-        quantize_w(1, 0, "w10_codes")
-        rest[1] = packed("rest1", S - SLICE, "w_raw10", 256)
-        first[1] = packed("first1", SLICE, "first1_codes")
-        for side, c0, c1, y0 in pieces:
-            grouped = x_bf_rest[1][:, c0:c1] if side is rest else x_bf_halves[c0 // P][:]
-            quantize(side[1][0][:, c0:c1], side[1][1][:, c0:c1], grouped)
-        for n, (side, c0, c1, y0) in enumerate(pieces):
-            multiply(acc0[n][:], 1, 0, side[1], c0, c1)
-        w_bf_last.append(reused.tile([P, half, PACK], BF16, name="w_bf_last1", align_bytes=256, offset=0))
-        interleave(nc.vector.tensor_copy, w_bf_last[1][:], w_raw[1, 1][:, :, half:])
-        w_mx[0, 1] = (reused.tile([P, P], U32, name="w01_codes", align_bytes=256, offset=512), keep.tile([P, P], U8, name="w01_scales", align_bytes=64))
-        quantize(w_mx[0, 1][0][:], w_mx[0, 1][1][:], w_bf[0, 1][:])
-        w_mx[1, 1] = packed("w11", P, "x_bf_half1")
-        for n in range(2):
-            quantize(w_mx[1, 1][0][:, n * half : (n + 1) * half], w_mx[1, 1][1][:, n * half : (n + 1) * half], w_bf_last[n][:])
-        for n, (side, c0, c1, y0) in enumerate(pieces):
-            if n == 2:
-                nc.vector.tensor_scalar_add(y[0][:, y0 : y0 + c1 - c0], acc0[n][:], bias[0][:])
-            else:
-                nc.scalar.activation(y[0][:, y0 : y0 + c1 - c0], acc0[n][:], IDENTITY, bias=bias[0][:])
-        acc1 = [psum.tile([P, c1 - c0], F32, name=f"acc1{n}", tag=f"acc0{n}") for n, (side, c0, c1, y0) in enumerate(pieces)]
+        pieces = [(0, WIDE), (WIDE, STEPPED), (STEPPED, STEPPED + P), (STEPPED + P, S)]
+        acc = {(h, n): psum.tile([P, c1 - c0], F32, name=f"acc{h}{n}") for h in range(BLOCKS) for n, (c0, c1) in enumerate(pieces)}
+        quantize_w(0, 0)
+        woven = tile("x_bf1_woven", [P, DENSE, PACK], BF16, "w_raw00")
+        weave(nc.vector.tensor_copy, woven[:], dense[:])
+        x_mx[1] = packed("x1", S, "w_bf00")
+        for n, (c0, c1) in enumerate(pieces):
+            multiply(acc[0, n][:], 0, 0, c0, c1)
+        for n, (c0, c1) in enumerate(pieces):
+            grouped = stepped[:, c0:c1] if c1 <= STEPPED else woven[:, c0 - STEPPED : c1 - STEPPED]
+            quantize(x_mx[1], c0, c1, grouped)
+            if n == 0:
+                quantize_w(1, 0)
+        for n, (c0, c1) in enumerate(pieces):
+            multiply(acc[0, n][:], 1, 0, c0, c1)
+        quantize_w(0, 1)
+        quantize_w(1, 1)
         for a in range(PASSES):
-            for n, (side, c0, c1, y0) in enumerate(pieces):
-                multiply(acc1[n][:], a, 1, side[a], c0, c1)
-        for n, (side, c0, c1, y0) in enumerate(pieces):
-            nc.scalar.activation(y[1][:, y0 : y0 + c1 - c0], acc1[n][:], IDENTITY, bias=bias[1][:])
+            for n, (c0, c1) in enumerate(pieces):
+                multiply(acc[1, n][:], a, 1, c0, c1)
+        y = [tile(f"y{h}", [P, S], F32) for h in range(BLOCKS)]
+        for h in range(BLOCKS):
+            for n, (c0, c1) in enumerate(pieces):
+                if (h, n) == (0, 2):
+                    nc.vector.tensor_scalar_add(y[h][:, c0:c1], acc[h, n][:], bias[h][:])
+                else:
+                    nc.scalar.activation(y[h][:, c0:c1], acc[h, n][:], IDENTITY, bias=bias[h][:])
+
+        cuts = [(0, WIDE), (WIDE, V)]
+        term = {(h, d): tile(f"term{h}{d}", [P, V], F32) for h in range(BLOCKS) for d in range(D)}
+        fetched = [tile("fetched0", [P, V], F32), tile("fetched1", [P, V - WIDE], F32)]
+        result = [tile(f"result{h}", [P, V], F32) for h in range(BLOCKS)]
+
+        def places(d, v0, v1):
+            return pos_sb[d][:, v0 // STRIPE : v1 // STRIPE]
+
+        def weighted(h, d, v0, v1):
+            nc.vector.tensor_tensor(term[h, d][:, v0:v1], y[h][:].indirect(places(d, v0, v1)), gate_sb[d][:, v0:v1], MULT)
+
+        def add(h, v0, v1):
+            nc.vector.tensor_tensor(result[h][:, v0:v1], term[h, 0][:, v0:v1], term[h, 1][:, v0:v1], ADD)
+
         weighted(0, 0, 0, V)
-        weighted(0, 1, 0, 256)
-        weighted(0, 1, 256, V)
-        weighted(1, 0, 0, V)
-        turned = keep.tile([P, 3, P], F32, name="turned", tag="bias1")
-        summed = keep.tile([P, 3, P], F32, name="summed", align_bytes=256)
-        sums = [psum.tile([P, P], F32, name=f"sums{c}") for c in range(2)] + [psum.tile([P, P], F32, name="sums2", tag="acc00")]
-        backs = [psum.tile([P, P], F32, name=f"backs{c}") for c in range(2)] + [psum.tile([P, P], F32, name="backs2", tag="acc01")]
-        for d in range(D):
-            for c in range(3):
-                nc.tensor.matmul(sums[c][:], term[0, d][:, c * P : (c + 1) * P], identity[:], start=(d == 0), stop=(d == D - 1), is_transpose=True)
-        for c in range(3):
-            nc.scalar.copy(turned[:, c], sums[c][:])
-        for c in range(3):
-            nc.tensor.transpose(backs[c][:], turned[:, c], identity[:])
-        for c in range(3):
-            nc.scalar.copy(summed[:, c], backs[c][:])
-        nc.scalar.dma_start(out[:P, : 2 * P], summed[:, :2].rearrange("p c v -> p (c v)"))
-        nc.scalar.dma_start(out[:P, 2 * P :], summed[:, 2])
-        weighted(1, 1, 0, 256)
-        weighted(1, 1, 256, V)
-        finish(1, 0, 256, "result_wide")
-        finish(1, 256, V, "result_last")
+        for v0, v1 in cuts:
+            weighted(0, 1, v0, v1)
+        for v0, v1 in cuts:
+            add(0, v0, v1)
+        nc.sync.dma_start(out[:P], result[0][:])
+        scalar_gather(fetched[0][:], y[1][:], pos_sb[0][:])
+        scalar_gather(fetched[1][:], y[1][:], places(1, WIDE, V))
+        weighted(1, 1, 0, WIDE)
+        nc.vector.tensor_tensor(term[1, 0][:], fetched[0][:], gate_sb[0][:], MULT)
+        nc.vector.tensor_tensor(term[1, 1][:, WIDE:], fetched[1][:], gate_sb[1][:, WIDE:], MULT)
+        for v0, v1 in cuts:
+            add(1, v0, v1)
+            nc.sync.dma_start(out[P:, v0:v1], result[1][:, v0:v1])

@@ -31,6 +31,7 @@ def tile_picked_sub_lin_bias_sub_e_kernel(tc, xT, w, b, gate, offs, pos1, pos2, 
     nc = tc.nc
     with ExitStack() as ctx:
         keep = ctx.enter_context(tc.tile_pool(name="keep", bufs=1))
+        held = ctx.enter_context(tc.tile_pool(name="held", bufs=1))
         psum = ctx.enter_context(tc.psum_pool(name="psum", bufs=1))
 
         def tile(name, shape, dtype, tag=None):
@@ -50,17 +51,16 @@ def tile_picked_sub_lin_bias_sub_e_kernel(tc, xT, w, b, gate, offs, pos1, pos2, 
                 nc.sync.dma_start(offs_sb[:], offs)
         w_rows = w.rearrange("(a p j) n -> a p j n", p=P, j=PACK)
         w_raw = {}
+        bias = [tile(f"bias{h}", [P, 1], F32) for h in range(BLOCKS)]
         for h in range(BLOCKS):
             for a in range(PASSES):
                 w_raw[a, h] = tile(f"w_raw{a}{h}", [P, PACK, P], F32)
                 nc.sync.dma_start(w_raw[a, h][:], w_rows[a][:, :, h * P : (h + 1) * P])
-        bias = [tile(f"bias{h}", [P, 1], F32) for h in range(BLOCKS)]
-        gate_sb = [tile(f"gate_sb{d}", [P, V], F32) for d in range(D)]
+        gate_sb = tile("gate_sb", [P, D, V], F32)
         nc.sync.dma_start(bias[0][:], b[:P])
         nc.sync.dma_start(pos_sb[0][:], pos1)
-        nc.sync.dma_start(gate_sb[0][:], gate[0, :P])
         nc.sync.dma_start(pos_sb[1][:], pos2)
-        nc.sync.dma_start(gate_sb[1][:], gate[1, :P])
+        nc.sync.dma_start(gate_sb[:], gate.rearrange("d m v -> m d v")[:P])
         nc.sync.dma_start(bias[1][:], b[P:])
 
         def offsets(c0, c1):
@@ -85,17 +85,23 @@ def tile_picked_sub_lin_bias_sub_e_kernel(tc, xT, w, b, gate, offs, pos1, pos2, 
             codes, scales = operand
             nc.vector.quantize_mx(out=codes[:, c0:c1].bitcast(FP8X4), scales=scales[:, c0:c1], in_=grouped.rearrange("p c t -> p (c t)"))
 
-        def packed(name, width, tag=None):
-            return tile(f"{name}_codes", [P, width], U32, tag), tile(f"{name}_scales", [P, width], U8)
+        def packed(name, width):
+            return tile(f"{name}_codes", [P, width], U32), tile(f"{name}_scales", [P, width], U8)
+
+        def placed(name, shape, dtype, offset):
+            return held.tile(shape, dtype, name=name, align_bytes=256, offset=offset)
 
         w_bf, w_mx, x_mx = {}, {}, {}
 
         def round_w(copy, a, h):
-            w_bf[a, h] = tile(f"w_bf{a}{h}", [P, P, PACK], BF16)
+            if (a, h) == (0, 0):
+                w_bf[a, h] = placed("w_bf00", [P, P, PACK], BF16, 2560)
+            else:
+                w_bf[a, h] = tile(f"w_bf{a}{h}", [P, P, PACK], BF16)
             weave(copy, w_bf[a, h][:], w_raw[a, h][:])
 
-        def quantize_w(a, h, tag=None):
-            w_mx[a, h] = packed(f"w{a}{h}", P, tag)
+        def quantize_w(a, h):
+            w_mx[a, h] = packed(f"w{a}{h}", P)
             quantize(w_mx[a, h], 0, P, w_bf[a, h][:])
 
         def multiply(acc, a, h, c0, c1):
@@ -134,31 +140,35 @@ def tile_picked_sub_lin_bias_sub_e_kernel(tc, xT, w, b, gate, offs, pos1, pos2, 
         for j in (2, 3):
             vector_gather(stepped[:, :, j], plane[1, j], offsets(0, STEPPED))
             scalar_gather(dense[:, j], plane[1, j], offsets(STEPPED, S))
-        for a, h in ((0, 0), (1, 0), (0, 1), (1, 1)):
-            round_w(nc.scalar.copy, a, h)
+        for a in range(PASSES):
+            round_w(nc.scalar.copy, a, 0)
 
         pieces = [(0, WIDE), (WIDE, STEPPED), (STEPPED, STEPPED + P), (STEPPED + P, S)]
         acc = {(h, n): psum.tile([P, c1 - c0], F32, name=f"acc{h}{n}") for h in range(BLOCKS) for n, (c0, c1) in enumerate(pieces)}
         quantize_w(0, 0)
-        woven = tile("x_bf1_woven", [P, DENSE, PACK], BF16, "w_raw00")
-        weave(nc.vector.tensor_copy, woven[:], dense[:])
-        x_mx[1] = packed("x1", S, "w_bf00")
+        woven = [tile("x_bf1_woven0", [P, P, PACK], BF16, "w_raw00"), placed("x_bf1_woven1", [P, P, PACK], BF16, 3072)]
+        weave(nc.vector.tensor_copy, woven[0][:], dense[:, :, :P])
+        weave(nc.scalar.copy, woven[1][:], dense[:, :, P:])
+        round_w(nc.scalar.copy, 0, 1)
+        x_mx[1] = (placed("x1_codes", [P, S], U32, 0), tile("x1_scales", [P, S], U8))
         for n, (c0, c1) in enumerate(pieces):
             multiply(acc[0, n][:], 0, 0, c0, c1)
         for n, (c0, c1) in enumerate(pieces):
-            grouped = stepped[:, c0:c1] if c1 <= STEPPED else woven[:, c0 - STEPPED : c1 - STEPPED]
+            grouped = stepped[:, c0:c1] if c1 <= STEPPED else woven[(c0 - STEPPED) // P][:]
             quantize(x_mx[1], c0, c1, grouped)
             if n == 0:
                 quantize_w(1, 0)
         for n, (c0, c1) in enumerate(pieces):
             multiply(acc[0, n][:], 1, 0, c0, c1)
+        round_w(nc.vector.tensor_copy, 1, 1)
         quantize_w(0, 1)
         quantize_w(1, 1)
         for a in range(PASSES):
             for n, (c0, c1) in enumerate(pieces):
                 multiply(acc[1, n][:], a, 1, c0, c1)
         y = [tile(f"y{h}", [P, S], F32) for h in range(BLOCKS)]
-        for h in range(BLOCKS):
+
+        def empty_banks(h):
             for n, (c0, c1) in enumerate(pieces):
                 if (h, n) == (0, 2):
                     nc.vector.tensor_scalar_add(y[h][:, c0:c1], acc[h, n][:], bias[h][:])
@@ -166,30 +176,34 @@ def tile_picked_sub_lin_bias_sub_e_kernel(tc, xT, w, b, gate, offs, pos1, pos2, 
                     nc.scalar.activation(y[h][:, c0:c1], acc[h, n][:], IDENTITY, bias=bias[h][:])
 
         cuts = [(0, WIDE), (WIDE, V)]
-        term = {(h, d): tile(f"term{h}{d}", [P, V], F32) for h in range(BLOCKS) for d in range(D)}
-        fetched = [tile("fetched0", [P, V], F32), tile("fetched1", [P, V - WIDE], F32)]
+        term = [tile(f"term{h}", [P, D, V], F32) for h in range(BLOCKS)]
+        fetched = tile("fetched", [P, D, V], F32)
         result = [tile(f"result{h}", [P, V], F32) for h in range(BLOCKS)]
 
         def places(d, v0, v1):
             return pos_sb[d][:, v0 // STRIPE : v1 // STRIPE]
 
         def weighted(h, d, v0, v1):
-            nc.vector.tensor_tensor(term[h, d][:, v0:v1], y[h][:].indirect(places(d, v0, v1)), gate_sb[d][:, v0:v1], MULT)
+            nc.vector.tensor_tensor(term[h][:, d, v0:v1], y[h][:].indirect(places(d, v0, v1)), gate_sb[:, d, v0:v1], MULT)
 
         def add(h, v0, v1):
-            nc.vector.tensor_tensor(result[h][:, v0:v1], term[h, 0][:, v0:v1], term[h, 1][:, v0:v1], ADD)
+            nc.vector.tensor_tensor(result[h][:, v0:v1], term[h][:, 0, v0:v1], term[h][:, 1, v0:v1], ADD)
 
+        empty_banks(0)
+        early = tile("early", [P, V - WIDE], F32)
+        scalar_gather(early[:], y[0][:], places(1, WIDE, V))
+        empty_banks(1)
         weighted(0, 0, 0, V)
-        for v0, v1 in cuts:
-            weighted(0, 1, v0, v1)
+        weighted(0, 1, 0, WIDE)
+        nc.vector.tensor_tensor(term[0][:, 1, WIDE:], early[:], gate_sb[:, 1, WIDE:], MULT)
         for v0, v1 in cuts:
             add(0, v0, v1)
         nc.sync.dma_start(out[:P], result[0][:])
-        scalar_gather(fetched[0][:], y[1][:], pos_sb[0][:])
-        scalar_gather(fetched[1][:], y[1][:], places(1, WIDE, V))
+        scalar_gather(fetched[:, 0], y[1][:], pos_sb[0][:])
+        scalar_gather(fetched[:, 1, WIDE:], y[1][:], places(1, WIDE, V))
         weighted(1, 1, 0, WIDE)
-        nc.vector.tensor_tensor(term[1, 0][:], fetched[0][:], gate_sb[0][:], MULT)
-        nc.vector.tensor_tensor(term[1, 1][:, WIDE:], fetched[1][:], gate_sb[1][:, WIDE:], MULT)
+        nc.vector.tensor_tensor(term[1][:, 0, :WIDE], fetched[:, 0, :WIDE], gate_sb[:, 0, :WIDE], MULT)
+        nc.vector.tensor_tensor(term[1][:, :, WIDE:], fetched[:, :, WIDE:], gate_sb[:, :, WIDE:], MULT)
         for v0, v1 in cuts:
             add(1, v0, v1)
             nc.sync.dma_start(out[P:, v0:v1], result[1][:, v0:v1])

@@ -1,6 +1,7 @@
 from contextlib import ExitStack
 
 import concourse.mybir as mybir
+from concourse.masks import make_identity
 
 K, T, D, S, V, N = 1024, 2048, 2, 768, 384, 256
 FLOPS = 2 * K * N * S
@@ -42,6 +43,8 @@ def tile_picked_sub_lin_bias_sub_e_kernel(tc, xT, w, b, gate, offs, pos1, pos2, 
 
         x_rows = xT.rearrange("(a p j) t -> a p j t", p=P, j=PACK)
         plane = {}
+        bias_rows = tile("bias_rows", [P, P], F32)
+        nc.vector.memset(bias_rows[:], 0.0)
         for a, j0, j1 in ((0, 0, 2), (0, 2, 4), (1, 0, 2), (1, 2, 3), (1, 3, 4)):
             loaded = tile(f"planes{a}{j0}", [P, (j1 - j0) * T], F32)
             nc.sync.dma_start(loaded[:], x_rows[a][:, j0:j1].rearrange("p j t -> p (j t)"))
@@ -49,19 +52,25 @@ def tile_picked_sub_lin_bias_sub_e_kernel(tc, xT, w, b, gate, offs, pos1, pos2, 
                 plane[a, j] = loaded[:, (j - j0) * T : (j - j0 + 1) * T]
             if (a, j0) == (0, 0):
                 nc.sync.dma_start(offs_sb[:], offs)
+                nc.sync.dma_start(bias_rows[:BLOCKS], b.rearrange("(h m) o -> h (m o)", h=BLOCKS))
         w_rows = w.rearrange("(a p j) n -> a p j n", p=P, j=PACK)
         w_raw = {}
-        bias = [tile(f"bias{h}", [P, 1], F32) for h in range(BLOCKS)]
         for h in range(BLOCKS):
             for a in range(PASSES):
                 w_raw[a, h] = tile(f"w_raw{a}{h}", [P, PACK, P], F32)
                 nc.sync.dma_start(w_raw[a, h][:], w_rows[a][:, :, h * P : (h + 1) * P])
         gate_sb = tile("gate_sb", [P, D, V], F32)
-        nc.sync.dma_start(bias[0][:], b[:P])
         nc.sync.dma_start(pos_sb[0][:], pos1)
         nc.sync.dma_start(pos_sb[1][:], pos2)
         nc.sync.dma_start(gate_sb[:], gate.rearrange("d m v -> m d v")[:P])
-        nc.sync.dma_start(bias[1][:], b[P:])
+
+        identity = keep.tile([P, P], F32, name="identity")
+        make_identity(nc, identity[:])
+        bias_turned = psum.tile([P, P], F32, name="bias_turned", tag="acc00")
+        nc.tensor.transpose(bias_turned[:], bias_rows[:], identity[:])
+        bias_sb = tile("bias_sb", [P, BLOCKS], F32)
+        nc.scalar.activation(bias_sb[:], bias_turned[:, :BLOCKS], IDENTITY)
+        bias = [bias_sb[:, h : h + 1] for h in range(BLOCKS)]
 
         def offsets(c0, c1):
             return offs_sb[:, c0 // STRIPE : c1 // STRIPE]
@@ -171,9 +180,9 @@ def tile_picked_sub_lin_bias_sub_e_kernel(tc, xT, w, b, gate, offs, pos1, pos2, 
         def empty_banks(h):
             for n, (c0, c1) in enumerate(pieces):
                 if (h, n) == (0, 2):
-                    nc.vector.tensor_scalar_add(y[h][:, c0:c1], acc[h, n][:], bias[h][:])
+                    nc.vector.tensor_scalar_add(y[h][:, c0:c1], acc[h, n][:], bias[h])
                 else:
-                    nc.scalar.activation(y[h][:, c0:c1], acc[h, n][:], IDENTITY, bias=bias[h][:])
+                    nc.scalar.activation(y[h][:, c0:c1], acc[h, n][:], IDENTITY, bias=bias[h])
 
         cuts = [(0, WIDE), (WIDE, V)]
         term = [tile(f"term{h}", [P, D, V], F32) for h in range(BLOCKS)]

@@ -23,8 +23,6 @@ K_PASS = P * PACK
 PASSES = K // K_PASS
 BLOCKS = N // P
 STRIPE = 16
-STEPPED = 512
-DENSE = S - STEPPED
 WIDE = 256
 
 
@@ -32,7 +30,6 @@ def tile_picked_sub_lin_bias_sub_e_kernel(tc, xT, w, b, gate, offs, pos1, pos2, 
     nc = tc.nc
     with ExitStack() as ctx:
         keep = ctx.enter_context(tc.tile_pool(name="keep", bufs=1))
-        held = ctx.enter_context(tc.tile_pool(name="held", bufs=1))
         psum = ctx.enter_context(tc.psum_pool(name="psum", bufs=1))
 
         def tile(name, shape, dtype, tag=None):
@@ -42,23 +39,31 @@ def tile_picked_sub_lin_bias_sub_e_kernel(tc, xT, w, b, gate, offs, pos1, pos2, 
         pos_sb = [keep.tile([P, V // STRIPE], U16, name=f"pos_sb{d}") for d in range(D)]
 
         x_rows = xT.rearrange("(a p j) t -> a p j t", p=P, j=PACK)
-        plane = {}
-        bias_rows = tile("bias_rows", [P, P], F32)
-        nc.vector.memset(bias_rows[:], 0.0)
-        for a, j0, j1 in ((0, 0, 2), (0, 2, 4), (1, 0, 2), (1, 2, 3), (1, 3, 4)):
+        w_rows = w.rearrange("(a p j) n -> a p j n", p=P, j=PACK)
+        plane, w_raw = {}, {}
+
+        def load_planes(a, j0, j1):
             loaded = tile(f"planes{a}{j0}", [P, (j1 - j0) * T], F32)
             nc.sync.dma_start(loaded[:], x_rows[a][:, j0:j1].rearrange("p j t -> p (j t)"))
             for j in range(j0, j1):
                 plane[a, j] = loaded[:, (j - j0) * T : (j - j0 + 1) * T]
-            if (a, j0) == (0, 0):
-                nc.sync.dma_start(offs_sb[:], offs)
-                nc.sync.dma_start(bias_rows[:BLOCKS], b.rearrange("(h m) o -> h (m o)", h=BLOCKS))
-        w_rows = w.rearrange("(a p j) n -> a p j n", p=P, j=PACK)
-        w_raw = {}
-        for h in range(BLOCKS):
-            for a in range(PASSES):
-                w_raw[a, h] = tile(f"w_raw{a}{h}", [P, PACK, P], F32)
-                nc.sync.dma_start(w_raw[a, h][:], w_rows[a][:, :, h * P : (h + 1) * P])
+
+        def load_w(a, h):
+            w_raw[a, h] = tile(f"w_raw{a}{h}", [P, PACK, P], F32)
+            nc.sync.dma_start(w_raw[a, h][:], w_rows[a][:, :, h * P : (h + 1) * P])
+
+        bias_rows = tile("bias_rows", [P, P], F32)
+        nc.vector.memset(bias_rows[:], 0.0)
+        load_planes(0, 0, 2)
+        nc.sync.dma_start(offs_sb[:], offs)
+        nc.sync.dma_start(bias_rows[:BLOCKS], b.rearrange("(h m) o -> h (m o)", h=BLOCKS))
+        load_planes(0, 2, 4)
+        load_w(0, 0)
+        for j in range(PACK):
+            load_planes(1, j, j + 1)
+        load_w(1, 0)
+        load_w(0, 1)
+        load_w(1, 1)
         gate_sb = tile("gate_sb", [P, D, V], F32)
         nc.sync.dma_start(pos_sb[0][:], pos1)
         nc.sync.dma_start(pos_sb[1][:], pos2)
@@ -97,33 +102,30 @@ def tile_picked_sub_lin_bias_sub_e_kernel(tc, xT, w, b, gate, offs, pos1, pos2, 
         def packed(name, width):
             return tile(f"{name}_codes", [P, width], U32), tile(f"{name}_scales", [P, width], U8)
 
-        def placed(name, shape, dtype, offset):
-            return held.tile(shape, dtype, name=name, align_bytes=256, offset=offset)
-
         w_bf, w_mx, x_mx = {}, {}, {}
 
         def round_w(copy, a, h):
-            if (a, h) == (0, 0):
-                w_bf[a, h] = placed("w_bf00", [P, P, PACK], BF16, 2560)
-            else:
-                w_bf[a, h] = tile(f"w_bf{a}{h}", [P, P, PACK], BF16)
+            w_bf[a, h] = tile(f"w_bf{a}{h}", [P, P, PACK], BF16)
             weave(copy, w_bf[a, h][:], w_raw[a, h][:])
 
         def quantize_w(a, h):
             w_mx[a, h] = packed(f"w{a}{h}", P)
             quantize(w_mx[a, h], 0, P, w_bf[a, h][:])
 
-        def multiply(acc, a, h, c0, c1):
-            codes, scales = x_mx[a]
+        def multiply(a, h, n):
+            codes, scales = x_mx[a, n]
             nc.tensor.matmul_mx(
-                out=acc,
+                out=acc[h, n][:],
                 lhsT=w_mx[a, h][0][:].bitcast(FP8X4),
                 lhsT_scale=w_mx[a, h][1][:],
-                rhs=codes[:, c0:c1].bitcast(FP8X4),
-                rhs_scale=scales[:, c0:c1],
+                rhs=codes[:].bitcast(FP8X4),
+                rhs_scale=scales[:],
                 start=(a == 0),
                 stop=(a == PASSES - 1),
             )
+
+        pieces = [(0, WIDE), (WIDE, WIDE + P), (WIDE + P, S - P), (S - P, S)]
+        acc = {(h, n): psum.tile([P, c1 - c0], F32, name=f"acc{h}{n}") for h in range(BLOCKS) for n, (c0, c1) in enumerate(pieces)}
 
         picked0 = tile("picked0", [P, PACK, S], F32)
         x_bf0 = [tile("x_bf0_first", [P, WIDE, PACK], BF16), tile("x_bf0_rest", [P, S - WIDE, PACK], BF16)]
@@ -133,60 +135,55 @@ def tile_picked_sub_lin_bias_sub_e_kernel(tc, xT, w, b, gate, offs, pos1, pos2, 
         scalar_gather(picked0[:, 3], plane[0, 3], offs_sb[:])
         weave_pair(scalar_round, x_bf0[0][:], 2, picked0[:, 2:, :WIDE])
         weave(nc.vector.tensor_copy, x_bf0[1][:], picked0[:, :, WIDE:])
-        x_mx[0] = packed("x0", S)
-        quantize(x_mx[0], 0, WIDE, x_bf0[0][:])
-        quantize(x_mx[0], WIDE, S, x_bf0[1][:])
-
-        stepped = tile("x_bf1_stepped", [P, STEPPED, PACK], BF16)
-        dense = tile("x_bf1_dense", [P, PACK, DENSE], BF16)
-        picked1 = [tile("picked1_stepped", [P, 2, STEPPED], F32), tile("picked1_dense", [P, 2, DENSE], F32)]
-        vector_gather(picked1[0][:, 0], plane[1, 0], offsets(0, STEPPED))
-        scalar_gather(picked1[0][:, 1], plane[1, 1], offsets(0, STEPPED))
-        weave_pair(nc.vector.tensor_copy, stepped[:], 0, picked1[0][:])
-        for j in range(2):
-            scalar_gather(picked1[1][:, j], plane[1, j], offsets(STEPPED, S))
-        nc.scalar.copy(dense[:, :2], picked1[1][:])
-        for j in (2, 3):
-            vector_gather(stepped[:, :, j], plane[1, j], offsets(0, STEPPED))
-            scalar_gather(dense[:, j], plane[1, j], offsets(STEPPED, S))
-        for a in range(PASSES):
-            round_w(nc.scalar.copy, a, 0)
-
-        pieces = [(0, WIDE), (WIDE, STEPPED), (STEPPED, STEPPED + P), (STEPPED + P, S)]
-        acc = {(h, n): psum.tile([P, c1 - c0], F32, name=f"acc{h}{n}") for h in range(BLOCKS) for n, (c0, c1) in enumerate(pieces)}
+        x0 = packed("x0", S)
+        quantize(x0, 0, WIDE, x_bf0[0][:])
+        quantize(x0, WIDE, S, x_bf0[1][:])
+        for n, (c0, c1) in enumerate(pieces):
+            x_mx[0, n] = (x0[0][:, c0:c1], x0[1][:, c0:c1])
+        round_w(nc.scalar.copy, 0, 0)
         quantize_w(0, 0)
-        woven = [tile("x_bf1_woven0", [P, P, PACK], BF16, "w_raw00"), placed("x_bf1_woven1", [P, P, PACK], BF16, 3072)]
-        weave(nc.vector.tensor_copy, woven[0][:], dense[:, :, :P])
-        weave(nc.scalar.copy, woven[1][:], dense[:, :, P:])
+        for n in range(len(pieces)):
+            multiply(0, 0, n)
+
+        x_bf1 = [tile(f"x_bf1{n}", [P, c1 - c0, PACK], BF16) for n, (c0, c1) in enumerate(pieces)]
+        for j in range(PACK):
+            for n, (c0, c1) in enumerate(pieces):
+                gather = vector_gather if n == 0 else scalar_gather
+                gather(x_bf1[n][:, :, j], plane[1, j], offsets(c0, c1))
+
+        def quantize_x1(n):
+            c0, c1 = pieces[n]
+            codes = tile(f"x1{n}_codes", [P, c1 - c0], U32, "x_bf11" if n == 0 else None)
+            x_mx[1, n] = (codes, tile(f"x1{n}_scales", [P, c1 - c0], U8))
+            quantize(x_mx[1, n], 0, c1 - c0, x_bf1[n][:])
+
+        quantize_x1(1)
+        round_w(nc.vector.tensor_copy, 1, 0)
+        quantize_x1(0)
+        quantize_w(1, 0)
+        quantize_x1(2)
+        quantize_x1(3)
+        for n in range(len(pieces)):
+            multiply(1, 0, n)
         round_w(nc.scalar.copy, 0, 1)
-        x_mx[1] = (placed("x1_codes", [P, S], U32, 0), tile("x1_scales", [P, S], U8))
-        for n, (c0, c1) in enumerate(pieces):
-            multiply(acc[0, n][:], 0, 0, c0, c1)
-        for n, (c0, c1) in enumerate(pieces):
-            grouped = stepped[:, c0:c1] if c1 <= STEPPED else woven[(c0 - STEPPED) // P][:]
-            quantize(x_mx[1], c0, c1, grouped)
-            if n == 0:
-                quantize_w(1, 0)
-        for n, (c0, c1) in enumerate(pieces):
-            multiply(acc[0, n][:], 1, 0, c0, c1)
         round_w(nc.vector.tensor_copy, 1, 1)
         quantize_w(0, 1)
         quantize_w(1, 1)
         for a in range(PASSES):
-            for n, (c0, c1) in enumerate(pieces):
-                multiply(acc[1, n][:], a, 1, c0, c1)
+            for n in range(len(pieces)):
+                multiply(a, 1, n)
         y = [tile(f"y{h}", [P, S], F32) for h in range(BLOCKS)]
 
         def empty_banks(h):
             for n, (c0, c1) in enumerate(pieces):
-                if (h, n) == (0, 2):
+                if (h, n) == (0, 3):
                     nc.vector.tensor_scalar_add(y[h][:, c0:c1], acc[h, n][:], bias[h])
                 else:
                     nc.scalar.activation(y[h][:, c0:c1], acc[h, n][:], IDENTITY, bias=bias[h])
 
         cuts = [(0, WIDE), (WIDE, V)]
         term = [tile(f"term{h}", [P, D, V], F32) for h in range(BLOCKS)]
-        fetched = tile("fetched", [P, D, V], F32)
+        fetched = tile("fetched", [P, V], F32)
         result = [tile(f"result{h}", [P, V], F32) for h in range(BLOCKS)]
 
         def places(d, v0, v1):
@@ -199,20 +196,20 @@ def tile_picked_sub_lin_bias_sub_e_kernel(tc, xT, w, b, gate, offs, pos1, pos2, 
             nc.vector.tensor_tensor(result[h][:, v0:v1], term[h][:, 0, v0:v1], term[h][:, 1, v0:v1], ADD)
 
         empty_banks(0)
-        early = tile("early", [P, V - WIDE], F32)
-        scalar_gather(early[:], y[0][:], places(1, WIDE, V))
+        early = tile("early", [P, WIDE], F32)
+        scalar_gather(early[:], y[0][:], places(1, 0, WIDE))
         empty_banks(1)
         weighted(0, 0, 0, V)
-        weighted(0, 1, 0, WIDE)
-        nc.vector.tensor_tensor(term[0][:, 1, WIDE:], early[:], gate_sb[:, 1, WIDE:], MULT)
-        for v0, v1 in cuts:
+        weighted(0, 1, WIDE, V)
+        nc.vector.tensor_tensor(term[0][:, 1, :WIDE], early[:], gate_sb[:, 1, :WIDE], MULT)
+        for v0, v1 in reversed(cuts):
             add(0, v0, v1)
         nc.sync.dma_start(out[:P], result[0][:])
-        scalar_gather(fetched[:, 0], y[1][:], pos_sb[0][:])
-        scalar_gather(fetched[:, 1, WIDE:], y[1][:], places(1, WIDE, V))
-        weighted(1, 1, 0, WIDE)
-        nc.vector.tensor_tensor(term[1][:, 0, :WIDE], fetched[:, 0, :WIDE], gate_sb[:, 0, :WIDE], MULT)
-        nc.vector.tensor_tensor(term[1][:, :, WIDE:], fetched[:, :, WIDE:], gate_sb[:, :, WIDE:], MULT)
+        for v0, v1 in cuts:
+            scalar_gather(fetched[:, v0:v1], y[1][:], places(0, v0, v1))
+        weighted(1, 1, 0, V)
+        for v0, v1 in cuts:
+            nc.vector.tensor_tensor(term[1][:, 0, v0:v1], fetched[:, v0:v1], gate_sb[:, 0, v0:v1], MULT)
         for v0, v1 in cuts:
             add(1, v0, v1)
             nc.sync.dma_start(out[P:, v0:v1], result[1][:, v0:v1])

@@ -24,6 +24,7 @@ PASSES = K // K_PASS
 BLOCKS = N // P
 STRIPE = 16
 WIDE = 256
+EARLY, LATE = 1, 0
 
 
 def tile_picked_sub_lin_bias_sub_e_kernel(tc, xT, w, b, gate, offs, pos1, pos2, out):
@@ -54,16 +55,19 @@ def tile_picked_sub_lin_bias_sub_e_kernel(tc, xT, w, b, gate, offs, pos1, pos2, 
 
         bias_rows = tile("bias_rows", [P, P], F32)
         nc.vector.memset(bias_rows[:], 0.0)
-        load_planes(0, 0, 2)
-        nc.sync.dma_start(offs_sb[:], offs)
+        load_planes(EARLY, 0, 3)
         nc.sync.dma_start(bias_rows[:BLOCKS], b.rearrange("(h m) o -> h (m o)", h=BLOCKS))
-        load_planes(0, 2, 4)
-        load_w(0, 0)
-        for j in range(PACK):
-            load_planes(1, j, j + 1)
-        load_w(1, 0)
-        load_w(0, 1)
-        load_w(1, 1)
+        nc.sync.dma_start(offs_sb[:], offs)
+        both = tile("planes_both", [P, PASSES * T], F32)
+        nc.sync.dma_start(both[:].rearrange("p (a t) -> p a t", a=PASSES), x_rows[:, :, 3].rearrange("a p t -> p a t"))
+        plane[LATE, 3] = both[:]
+        plane[EARLY, 3] = both[:, T:]
+        load_w(EARLY, 0)
+        for j in range(3):
+            load_planes(LATE, j, j + 1)
+        load_w(LATE, 0)
+        load_w(EARLY, 1)
+        load_w(LATE, 1)
         gate_sb = tile("gate_sb", [P, D, V], F32)
         nc.sync.dma_start(pos_sb[0][:], pos1)
         nc.sync.dma_start(pos_sb[1][:], pos2)
@@ -120,56 +124,58 @@ def tile_picked_sub_lin_bias_sub_e_kernel(tc, xT, w, b, gate, offs, pos1, pos2, 
                 lhsT_scale=w_mx[a, h][1][:],
                 rhs=codes[:].bitcast(FP8X4),
                 rhs_scale=scales[:],
-                start=(a == 0),
-                stop=(a == PASSES - 1),
+                start=(a == EARLY),
+                stop=(a == LATE),
             )
 
         pieces = [(0, WIDE), (WIDE, WIDE + P), (WIDE + P, S - P), (S - P, S)]
         acc = {(h, n): psum.tile([P, c1 - c0], F32, name=f"acc{h}{n}") for h in range(BLOCKS) for n, (c0, c1) in enumerate(pieces)}
 
-        picked0 = tile("picked0", [P, PACK, S], F32)
-        x_bf0 = [tile("x_bf0_first", [P, WIDE, PACK], BF16), tile("x_bf0_rest", [P, S - WIDE, PACK], BF16)]
-        for j in range(3):
-            vector_gather(picked0[:, j], plane[0, j], offs_sb[:])
-        weave_pair(scalar_round, x_bf0[0][:], 0, picked0[:, :2, :WIDE])
-        scalar_gather(picked0[:, 3], plane[0, 3], offs_sb[:])
-        weave_pair(scalar_round, x_bf0[0][:], 2, picked0[:, 2:, :WIDE])
-        weave(nc.vector.tensor_copy, x_bf0[1][:], picked0[:, :, WIDE:])
-        x0 = packed("x0", S)
-        quantize(x0, 0, WIDE, x_bf0[0][:])
-        quantize(x0, WIDE, S, x_bf0[1][:])
+        picked = tile("picked", [P, 2, S], F32)
+        x_early = tile("x_early", [P, S, PACK], BF16)
+        vector_gather(picked[:, 0], plane[EARLY, 0], offs_sb[:])
+        scalar_gather(picked[:, 1], plane[EARLY, 1], offs_sb[:])
+        vector_gather(x_early[:, :, 2], plane[EARLY, 2], offs_sb[:])
+        weave_pair(scalar_round, x_early[:, WIDE:], 0, picked[:, :, WIDE:])
+        weave_pair(nc.vector.tensor_copy, x_early[:, :WIDE], 0, picked[:, :, :WIDE])
+        vector_gather(x_early[:, :, 3], plane[EARLY, 3], offs_sb[:])
+        early_mx = packed("x_early", S)
+        quantize(early_mx, 0, WIDE, x_early[:, :WIDE])
+        quantize(early_mx, WIDE, S, x_early[:, WIDE:])
         for n, (c0, c1) in enumerate(pieces):
-            x_mx[0, n] = (x0[0][:, c0:c1], x0[1][:, c0:c1])
-        round_w(nc.scalar.copy, 0, 0)
-        quantize_w(0, 0)
+            x_mx[EARLY, n] = (early_mx[0][:, c0:c1], early_mx[1][:, c0:c1])
+        round_w(nc.scalar.copy, EARLY, 0)
+        quantize_w(EARLY, 0)
         for n in range(len(pieces)):
-            multiply(0, 0, n)
+            multiply(EARLY, 0, n)
 
-        x_bf1 = [tile(f"x_bf1{n}", [P, c1 - c0, PACK], BF16) for n, (c0, c1) in enumerate(pieces)]
-        for j in range(PACK):
+        x_late = [tile(f"x_late{n}", [P, c1 - c0, PACK], BF16) for n, (c0, c1) in enumerate(pieces)]
+        for j in (3, 0, 1, 2):
             for n, (c0, c1) in enumerate(pieces):
-                gather = vector_gather if n == 0 else scalar_gather
-                gather(x_bf1[n][:, :, j], plane[1, j], offsets(c0, c1))
+                if n == 0:
+                    vector_gather(x_late[n][:, :, j], plane[LATE, j][:, :T], offsets(c0, c1))
+                else:
+                    scalar_gather(x_late[n][:, :, j], plane[LATE, j], offsets(c0, c1))
 
-        def quantize_x1(n):
+        def quantize_late(n):
             c0, c1 = pieces[n]
-            codes = tile(f"x1{n}_codes", [P, c1 - c0], U32, "x_bf11" if n == 0 else None)
-            x_mx[1, n] = (codes, tile(f"x1{n}_scales", [P, c1 - c0], U8))
-            quantize(x_mx[1, n], 0, c1 - c0, x_bf1[n][:])
+            codes = tile(f"x_late{n}_codes", [P, c1 - c0], U32, "x_late1" if n == 0 else None)
+            x_mx[LATE, n] = (codes, tile(f"x_late{n}_scales", [P, c1 - c0], U8))
+            quantize(x_mx[LATE, n], 0, c1 - c0, x_late[n][:])
 
-        quantize_x1(1)
-        round_w(nc.vector.tensor_copy, 1, 0)
-        quantize_x1(0)
-        quantize_w(1, 0)
-        quantize_x1(2)
-        quantize_x1(3)
+        quantize_late(1)
+        round_w(nc.vector.tensor_copy, LATE, 0)
+        quantize_late(0)
+        quantize_w(LATE, 0)
+        quantize_late(2)
+        quantize_late(3)
         for n in range(len(pieces)):
-            multiply(1, 0, n)
-        round_w(nc.scalar.copy, 0, 1)
-        round_w(nc.vector.tensor_copy, 1, 1)
-        quantize_w(0, 1)
-        quantize_w(1, 1)
-        for a in range(PASSES):
+            multiply(LATE, 0, n)
+        round_w(nc.scalar.copy, EARLY, 1)
+        round_w(nc.vector.tensor_copy, LATE, 1)
+        quantize_w(EARLY, 1)
+        quantize_w(LATE, 1)
+        for a in (EARLY, LATE):
             for n in range(len(pieces)):
                 multiply(a, 1, n)
         y = [tile(f"y{h}", [P, S], F32) for h in range(BLOCKS)]
@@ -182,7 +188,7 @@ def tile_picked_sub_lin_bias_sub_e_kernel(tc, xT, w, b, gate, offs, pos1, pos2, 
                     nc.scalar.activation(y[h][:, c0:c1], acc[h, n][:], IDENTITY, bias=bias[h])
 
         cuts = [(0, WIDE), (WIDE, V)]
-        term = [tile(f"term{h}", [P, D, V], F32) for h in range(BLOCKS)]
+        term = [tile("term0", [P, D, V], F32), tile("term1", [P, D, V], F32, "y0")]
         fetched = tile("fetched", [P, V], F32)
         result = [tile(f"result{h}", [P, V], F32) for h in range(BLOCKS)]
 
@@ -200,9 +206,9 @@ def tile_picked_sub_lin_bias_sub_e_kernel(tc, xT, w, b, gate, offs, pos1, pos2, 
         scalar_gather(early[:], y[0][:], places(1, 0, WIDE))
         empty_banks(1)
         weighted(0, 0, 0, V)
-        weighted(0, 1, WIDE, V)
         nc.vector.tensor_tensor(term[0][:, 1, :WIDE], early[:], gate_sb[:, 1, :WIDE], MULT)
-        for v0, v1 in reversed(cuts):
+        weighted(0, 1, WIDE, V)
+        for v0, v1 in cuts:
             add(0, v0, v1)
         nc.sync.dma_start(out[:P], result[0][:])
         for v0, v1 in cuts:

@@ -71,7 +71,8 @@ def tile_picked_sub_lin_bias_sub_e_kernel(tc, xT, w, b, gate, offs, pos1, pos2, 
         gate_sb = tile("gate_sb", [P, D, V], F32)
         nc.sync.dma_start(pos_sb[0][:], pos1)
         nc.sync.dma_start(pos_sb[1][:], pos2)
-        nc.sync.dma_start(gate_sb[:], gate.rearrange("d m v -> m d v")[:P])
+        for d in range(D):
+            nc.sync.dma_start(gate_sb[:, d], gate[d, :P])
 
         identity = keep.tile([P, P], F32, name="identity")
         make_identity(nc, identity[:])
@@ -211,11 +212,22 @@ def tile_picked_sub_lin_bias_sub_e_kernel(tc, xT, w, b, gate, offs, pos1, pos2, 
         for v0, v1 in cuts:
             add(0, v0, v1)
         nc.sync.dma_start(out[:P], result[0][:])
-        for v0, v1 in cuts:
-            scalar_gather(fetched[:, v0:v1], y[1][:], places(0, v0, v1))
-        weighted(1, 1, 0, V)
-        for v0, v1 in cuts:
+        thirds = [(v0, v0 + P) for v0 in range(0, V, P)]
+
+        def weigh_fetched(v0, v1):
             nc.vector.tensor_tensor(term[1][:, 0, v0:v1], fetched[:, v0:v1], gate_sb[:, 0, v0:v1], MULT)
-        for v0, v1 in cuts:
+
+        def finish(v0, v1):
             add(1, v0, v1)
             nc.sync.dma_start(out[P:, v0:v1], result[1][:, v0:v1])
+
+        for v0, v1 in thirds:
+            scalar_gather(fetched[:, v0:v1], y[1][:], places(0, v0, v1))
+        weighted(1, 1, 0, WIDE)
+        weigh_fetched(*thirds[0])
+        weighted(1, 1, WIDE, V)
+        finish(*thirds[0])
+        for third in thirds[1:]:
+            weigh_fetched(*third)
+        for third in thirds[1:]:
+            finish(*third)

from contextlib import ExitStack

import concourse.mybir as mybir
from concourse.masks import make_identity

K, T, D, S, V, N = 1024, 2048, 2, 768, 384, 256
FLOPS = 2 * K * N * S

F32 = mybir.dt.float32
BF16 = mybir.dt.bfloat16
U32 = mybir.dt.uint32
U16 = mybir.dt.uint16
U8 = mybir.dt.uint8
FP8X4 = mybir.dt.float8_e4m3fn_x4
IDENTITY = mybir.ActivationFunctionType.Identity
COPY = mybir.ActivationFunctionType.Copy
ADD = mybir.AluOpType.add
MULT = mybir.AluOpType.mult

P = 128
PACK = 4
K_PASS = P * PACK
PASSES = K // K_PASS
BLOCKS = N // P
STRIPE = 16
WIDE = 256
EARLY, LATE = 1, 0


def tile_picked_sub_lin_bias_sub_e_kernel(tc, xT, w, b, gate, offs, pos1, pos2, out):
    nc = tc.nc
    with ExitStack() as ctx:
        keep = ctx.enter_context(tc.tile_pool(name="keep", bufs=1))
        psum = ctx.enter_context(tc.psum_pool(name="psum", bufs=1))

        def tile(name, shape, dtype, tag=None):
            return keep.tile(shape, dtype, name=name, tag=tag or name, align_bytes=256)

        offs_sb = keep.tile([P, S // STRIPE], U16, name="offs_sb")
        pos_sb = [keep.tile([P, V // STRIPE], U16, name=f"pos_sb{d}") for d in range(D)]

        x_rows = xT.rearrange("(a p j) t -> a p j t", p=P, j=PACK)
        w_rows = w.rearrange("(a p j) n -> a p j n", p=P, j=PACK)
        plane, w_raw = {}, {}

        def load_planes(a, j0, j1):
            loaded = tile(f"planes{a}{j0}", [P, (j1 - j0) * T], F32)
            nc.sync.dma_start(loaded[:], x_rows[a][:, j0:j1].rearrange("p j t -> p (j t)"))
            for j in range(j0, j1):
                plane[a, j] = loaded[:, (j - j0) * T : (j - j0 + 1) * T]

        def load_w(a, h):
            w_raw[a, h] = tile(f"w_raw{a}{h}", [P, PACK, P], F32)
            nc.sync.dma_start(w_raw[a, h][:], w_rows[a][:, :, h * P : (h + 1) * P])

        bias_rows = tile("bias_rows", [P, P], F32)
        nc.vector.memset(bias_rows[:], 0.0)
        load_planes(EARLY, 0, 3)
        nc.sync.dma_start(bias_rows[:BLOCKS], b.rearrange("(h m) o -> h (m o)", h=BLOCKS))
        nc.sync.dma_start(offs_sb[:], offs)
        both = tile("planes_both", [P, PASSES * T], F32)
        nc.sync.dma_start(both[:].rearrange("p (a t) -> p a t", a=PASSES), x_rows[:, :, 3].rearrange("a p t -> p a t"))
        plane[LATE, 3] = both[:]
        plane[EARLY, 3] = both[:, T:]
        load_w(EARLY, 0)
        for j in range(3):
            load_planes(LATE, j, j + 1)
        load_w(LATE, 0)
        load_w(EARLY, 1)
        load_w(LATE, 1)
        gate_sb = tile("gate_sb", [P, D, V], F32)
        nc.sync.dma_start(pos_sb[0][:], pos1)
        nc.sync.dma_start(pos_sb[1][:], pos2)
        for d in range(D):
            nc.sync.dma_start(gate_sb[:, d], gate[d, :P])

        identity = keep.tile([P, P], F32, name="identity")
        make_identity(nc, identity[:])
        bias_turned = psum.tile([P, P], F32, name="bias_turned", tag="acc00")
        nc.tensor.transpose(bias_turned[:], bias_rows[:], identity[:])
        bias_sb = tile("bias_sb", [P, BLOCKS], F32)
        nc.scalar.activation(bias_sb[:], bias_turned[:, :BLOCKS], IDENTITY)
        bias = [bias_sb[:, h : h + 1] for h in range(BLOCKS)]

        def offsets(c0, c1):
            return offs_sb[:, c0 // STRIPE : c1 // STRIPE]

        def vector_gather(dst, window, where):
            nc.vector.tensor_copy(dst, window.indirect(where))

        def scalar_gather(dst, window, where):
            nc.scalar.activation(dst, window.indirect(where), COPY)

        def scalar_round(dst, src):
            nc.scalar.activation(dst, src, IDENTITY)

        def weave(copy, dst, src):
            copy(dst.rearrange("p (c i) t -> p c t i", i=4), src.rearrange("p t (c i) -> p c t i", i=4))

        def weave_pair(copy, dst, j0, src):
            copy(dst[:, :, j0 : j0 + 2], src.rearrange("p t c -> p c t"))

        def quantize(operand, c0, c1, grouped):
            codes, scales = operand
            nc.vector.quantize_mx(out=codes[:, c0:c1].bitcast(FP8X4), scales=scales[:, c0:c1], in_=grouped.rearrange("p c t -> p (c t)"))

        def packed(name, width):
            return tile(f"{name}_codes", [P, width], U32), tile(f"{name}_scales", [P, width], U8)

        w_bf, w_mx, x_mx = {}, {}, {}

        def round_w(copy, a, h):
            w_bf[a, h] = tile(f"w_bf{a}{h}", [P, P, PACK], BF16)
            weave(copy, w_bf[a, h][:], w_raw[a, h][:])

        def quantize_w(a, h):
            w_mx[a, h] = packed(f"w{a}{h}", P)
            quantize(w_mx[a, h], 0, P, w_bf[a, h][:])

        def multiply(a, h, n):
            codes, scales = x_mx[a, n]
            nc.tensor.matmul_mx(
                out=acc[h, n][:],
                lhsT=w_mx[a, h][0][:].bitcast(FP8X4),
                lhsT_scale=w_mx[a, h][1][:],
                rhs=codes[:].bitcast(FP8X4),
                rhs_scale=scales[:],
                start=(a == EARLY),
                stop=(a == LATE),
            )

        pieces = [(0, WIDE), (WIDE, WIDE + P), (WIDE + P, S - P), (S - P, S)]
        acc = {(h, n): psum.tile([P, c1 - c0], F32, name=f"acc{h}{n}") for h in range(BLOCKS) for n, (c0, c1) in enumerate(pieces)}

        picked = tile("picked", [P, 2, S], F32)
        x_early = tile("x_early", [P, S, PACK], BF16)
        vector_gather(picked[:, 0], plane[EARLY, 0], offs_sb[:])
        scalar_gather(picked[:, 1], plane[EARLY, 1], offs_sb[:])
        vector_gather(x_early[:, :, 2], plane[EARLY, 2], offs_sb[:])
        weave_pair(scalar_round, x_early[:, WIDE:], 0, picked[:, :, WIDE:])
        weave_pair(nc.vector.tensor_copy, x_early[:, :WIDE], 0, picked[:, :, :WIDE])
        vector_gather(x_early[:, :, 3], plane[EARLY, 3], offs_sb[:])
        early_mx = packed("x_early", S)
        quantize(early_mx, 0, WIDE, x_early[:, :WIDE])
        quantize(early_mx, WIDE, S, x_early[:, WIDE:])
        for n, (c0, c1) in enumerate(pieces):
            x_mx[EARLY, n] = (early_mx[0][:, c0:c1], early_mx[1][:, c0:c1])
        round_w(nc.scalar.copy, EARLY, 0)
        quantize_w(EARLY, 0)
        for n in range(len(pieces)):
            multiply(EARLY, 0, n)

        x_late = [tile(f"x_late{n}", [P, c1 - c0, PACK], BF16) for n, (c0, c1) in enumerate(pieces)]
        for j in (3, 0, 1, 2):
            for n, (c0, c1) in enumerate(pieces):
                if n == 0:
                    vector_gather(x_late[n][:, :, j], plane[LATE, j][:, :T], offsets(c0, c1))
                else:
                    scalar_gather(x_late[n][:, :, j], plane[LATE, j], offsets(c0, c1))

        def quantize_late(n):
            c0, c1 = pieces[n]
            codes = tile(f"x_late{n}_codes", [P, c1 - c0], U32, "x_late1" if n == 0 else None)
            x_mx[LATE, n] = (codes, tile(f"x_late{n}_scales", [P, c1 - c0], U8))
            quantize(x_mx[LATE, n], 0, c1 - c0, x_late[n][:])

        quantize_late(1)
        round_w(nc.vector.tensor_copy, LATE, 0)
        quantize_late(0)
        quantize_w(LATE, 0)
        quantize_late(2)
        quantize_late(3)
        for n in range(len(pieces)):
            multiply(LATE, 0, n)
        round_w(nc.scalar.copy, EARLY, 1)
        round_w(nc.vector.tensor_copy, LATE, 1)
        quantize_w(EARLY, 1)
        quantize_w(LATE, 1)
        for a in (EARLY, LATE):
            for n in range(len(pieces)):
                multiply(a, 1, n)
        y = [tile(f"y{h}", [P, S], F32) for h in range(BLOCKS)]

        def empty_banks(h):
            for n, (c0, c1) in enumerate(pieces):
                if (h, n) == (0, 3):
                    nc.vector.tensor_scalar_add(y[h][:, c0:c1], acc[h, n][:], bias[h])
                else:
                    nc.scalar.activation(y[h][:, c0:c1], acc[h, n][:], IDENTITY, bias=bias[h])

        cuts = [(0, WIDE), (WIDE, V)]
        term = [tile("term0", [P, D, V], F32), tile("term1", [P, D, V], F32, "y0")]
        fetched = tile("fetched", [P, V], F32)
        result = [tile(f"result{h}", [P, V], F32) for h in range(BLOCKS)]

        def places(d, v0, v1):
            return pos_sb[d][:, v0 // STRIPE : v1 // STRIPE]

        def weighted(h, d, v0, v1):
            nc.vector.tensor_tensor(term[h][:, d, v0:v1], y[h][:].indirect(places(d, v0, v1)), gate_sb[:, d, v0:v1], MULT)

        def add(h, v0, v1):
            nc.vector.tensor_tensor(result[h][:, v0:v1], term[h][:, 0, v0:v1], term[h][:, 1, v0:v1], ADD)

        empty_banks(0)
        early = tile("early", [P, WIDE], F32)
        scalar_gather(early[:], y[0][:], places(1, 0, WIDE))
        empty_banks(1)
        weighted(0, 0, 0, V)
        nc.vector.tensor_tensor(term[0][:, 1, :WIDE], early[:], gate_sb[:, 1, :WIDE], MULT)
        weighted(0, 1, WIDE, V)
        for v0, v1 in cuts:
            add(0, v0, v1)
        nc.sync.dma_start(out[:P], result[0][:])
        thirds = [(v0, v0 + P) for v0 in range(0, V, P)]

        def weigh_fetched(v0, v1):
            nc.vector.tensor_tensor(term[1][:, 0, v0:v1], fetched[:, v0:v1], gate_sb[:, 0, v0:v1], MULT)

        def finish(v0, v1):
            add(1, v0, v1)
            nc.sync.dma_start(out[P:, v0:v1], result[1][:, v0:v1])

        for v0, v1 in thirds:
            scalar_gather(fetched[:, v0:v1], y[1][:], places(0, v0, v1))
        weighted(1, 1, 0, WIDE)
        weigh_fetched(*thirds[0])
        weighted(1, 1, WIDE, V)
        finish(*thirds[0])
        for third in thirds[1:]:
            weigh_fetched(*third)
        for third in thirds[1:]:
            finish(*third)
